import numpy as np
import ml_dtypes


def mxq(x, axis, fmt="e4m3"):
    dtype, down = {"e4m3": (ml_dtypes.float8_e4m3fn, 7), "e5m2": (ml_dtypes.float8_e5m2, 14)}[fmt]
    v = np.moveaxis(np.asarray(x, np.float32).astype(ml_dtypes.bfloat16).astype(np.float64), axis, -1)
    blocks = v.reshape(v.shape[:-1] + (-1, 32))
    amax = np.abs(blocks).max(-1, keepdims=True)
    byte = np.maximum(np.where(amax > 0, np.frexp(amax)[1] - 1 + 127, 0) - down, 1)
    scale = np.exp2(byte - 127.0)
    codes = (blocks / scale).astype(np.float32).astype(dtype).astype(np.float64)
    return np.moveaxis((codes * scale).reshape(v.shape), -1, axis)


WIDE = False


def mx_kscale(k):
    if not WIDE:
        return np.ones(k)
    levels = np.array([18, -18])
    if k % 512:
        return np.exp2(np.random.permutation(np.resize(levels, k // 32))).repeat(32)
    a = np.empty((k // 512, 16))
    for p in range(k // 512):
        a[p, :8] = np.random.permutation(np.resize(levels, 8))
        for g in range(8):
            far = levels[np.abs(levels - a[p, g]) >= 10]
            a[p, g + 8] = far[np.random.randint(len(far))]
    return np.exp2(a.ravel()).repeat(32)


def f64(x):
    return np.asarray(x).astype(np.float64)


def striped(idx):
    return np.tile(np.asarray(idx).reshape(-1, 16).T, (8, 1)).astype(np.uint16)


def unstriped(offs):
    return offs[:16].T.reshape(-1).astype(np.int64)


B, N, T, D, DV, R = 1, 512, 2048, 512, 512, 512


def setup_inputs():
    n = np.random.standard_normal
    idx = np.random.permutation(T)[:B * N]
    s = mx_kscale(D)[:, None]
    z = mx_kscale(R)[:, None]
    v = mx_kscale(DV)[:, None]
    q = n((B, D, R))
    do = n((B, DV, R))
    u = np.ones(T)
    u[idx] = mx_kscale(B * N)
    r = np.random.uniform(0.5, 2.0, T) * u
    return {
        "qT": (q * s).astype(np.float32),
        "kT": (n((D, T)) * (0.50 / np.sqrt(D)) / s / r).astype(np.float32),
        "vT": (n((DV, T)) / np.sqrt(DV) / v).astype(np.float32),
        "doT": (do * v).astype(np.float32),
        "lse": (np.log(N) + 0.12 + 0.1 * n((B, R, 1))).astype(np.float32),
        "delta": (0.3 * n((B, R, 1))).astype(np.float32),
        "rw": (np.random.uniform(0.5, 1.5, (B, R, 1)) * N / np.sqrt(R) * z).astype(np.float32),
        "ts": np.tile(r, (128, 1)).astype(np.float32),
        "qm": (q.transpose(0, 2, 1) / z).astype(np.float32),
        "offs": striped(idx),
    }


def reference(qT, kT, vT, doT, lse, delta, rw, ts, qm, offs):
    idx = unstriped(offs)
    pick = lambda x: x[:, idx].reshape(x.shape[0], B, N).transpose(1, 0, 2)
    k = pick(f64(kT))
    a = mxq(f64(qT), 1, "e4m3").transpose(0, 2, 1) @ mxq(k, 1, "e4m3")
    ts_ = pick(f64(ts))[:, :1, :]
    a = a * ts_
    p = np.exp(a - f64(lse))
    dp = mxq(f64(doT), 1, "e5m2").transpose(0, 2, 1) @ mxq(pick(f64(vT)), 1, "e4m3")
    ds = f64(rw) * p * (dp - f64(delta))
    ds = ts_ * ds
    gq = mxq(ds, 2, "e5m2") @ mxq(k, 2, "e4m3").transpose(0, 2, 1)
    dk = mxq(f64(qm), 1, "e4m3").transpose(0, 2, 1) @ mxq(ds, 1, "e5m2")
    gk = np.zeros((D, T))
    gk[:, idx] = dk.transpose(1, 0, 2).reshape(D, B * N)
    return gq, gk

@@ -1,0 +1,259 @@
+from contextlib import ExitStack
+
+import concourse.mybir as mybir
+from concourse.masks import make_identity
+
+N, T, D, DV, R = 512, 2048, 512, 512, 512
+FLOPS = 2 * R * N * (D + DV + D + D)
+
+F32 = mybir.dt.float32
+BF16 = mybir.dt.bfloat16
+U32 = mybir.dt.uint32
+U16 = mybir.dt.uint16
+U8 = mybir.dt.uint8
+E4 = mybir.dt.float8_e4m3fn_x4
+E5 = mybir.dt.float8_e5m2_x4
+ACT = mybir.ActivationFunctionType
+ALU = mybir.AluOpType
+
+P = 128
+PACK = 4
+DS_SPLIT = 352
+
+
+def tile_attend_gat_lse_qk_ts_kernel(
+    tc, qT, kT, vT, doT, lse, delta, rw, ts, qm, offs, out_0, out_1
+):
+    nc = tc.nc
+    with ExitStack() as ctx:
+        keep = ctx.enter_context(tc.tile_pool(name="keep", bufs=1))
+        psum = ctx.enter_context(tc.psum_pool(name="psum", bufs=4))
+
+        def sb(name, shape, dtype, tag=None):
+            return keep.tile(shape, dtype, name=name, tag=tag or name, align_bytes=64)
+
+        def bank(tag):
+            return psum.tile([P, 512], F32, name=tag, tag=tag)
+
+        def mx_tiles(name, tag=None):
+            return sb(name + "_codes", [P, 512], U32, tag), sb(name + "_scales", [P, 512], U8)
+
+        def quantize(mx, fmt, src, c0, c1):
+            nc.vector.quantize_mx(
+                out=mx[0][:, c0:c1].bitcast(fmt), scales=mx[1][:, c0:c1], in_=src[:, PACK * c0 : PACK * c1]
+            )
+
+        def matmul(out, stat, stat_fmt, block, mov, mov_fmt):
+            cols = slice(P * block, P * (block + 1))
+            nc.tensor.matmul_mx(
+                out=out[:],
+                lhsT=stat[0][:, cols].bitcast(stat_fmt),
+                lhsT_scale=stat[1][:, cols],
+                rhs=mov[0][:].bitcast(mov_fmt),
+                rhs_scale=mov[1][:],
+                start=True,
+                stop=True,
+            )
+
+        def interleave_views(dst, src, c0, c1):
+            out = dst[:, PACK * c0 : PACK * c1].rearrange("p (c i j) -> p c j i", i=4, j=PACK)
+            return out, src[:, :, c0:c1].rearrange("p j (c i) -> p c j i", i=4)
+
+        def query_views(dst, src, m0, m1):
+            out = dst[:].rearrange("p (t m j) -> p m j t", t=PACK, j=PACK)[:, m0:m1]
+            return out, src.rearrange("p j (m t) -> p m j t", t=PACK)
+
+        offsets = keep.tile([P, N // 16], U16, name="offsets")
+        nc.sync.dma_start(offsets[:], offs)
+        k_rows = kT.rearrange("(p j) t -> p j t", j=PACK)
+        v_rows = vT.rearrange("(p j) t -> p j t", j=PACK)
+        k_pool = [sb("k_pool%d" % j, [P, T], F32) for j in range(PACK)]
+        v_pool = [sb("v_pool%d" % j, [P, T], F32) for j in range(2)]
+        v_pool_hi = sb("v_pool_hi", [P, 2, T], F32)
+        q_raw = [sb("q_raw%d" % h, [P, PACK, R // 2], F32) for h in range(2)]
+        do_raw = sb("do_raw", [P, PACK, R], F32)
+        qm_raw = sb("qm_raw", [P, PACK, D], F32)
+        ts_pool = sb("ts_pool", [P, T], F32)
+        nc.vector.memset(ts_pool[:, 0 : T // 2], 0.0)
+        nc.gpsimd.memset(ts_pool[:, T // 2 : T], 0.0)
+        nc.sync.dma_start(ts_pool[0:1, :], ts[0:1, :])
+        lse_c = sb("lse_c", [P, PACK], F32)
+        delta_c = sb("delta_c", [P, PACK], F32)
+        rw_c = sb("rw_c", [P, PACK], F32)
+        for h in range(2):
+            half = slice(h * T // 2, (h + 1) * T // 2)
+            nc.sync.dma_start(k_pool[0][:, half], k_rows[:, 0, half])
+        for tile, src in ((lse_c, lse), (delta_c, delta), (rw_c, rw)):
+            nc.sync.dma_start(tile[:], src[0].rearrange("(p t) o -> p (t o)", t=PACK))
+        for h in range(2):
+            half = slice(h * T // 2, (h + 1) * T // 2)
+            nc.sync.dma_start(k_pool[1][:, half], k_rows[:, 1, half])
+        for j in range(2, PACK):
+            nc.sync.dma_start(k_pool[j][:], k_rows[:, j, :])
+        q_rows = qT[0].rearrange("(p j) r -> p j r", j=PACK)
+        for h in range(2):
+            nc.sync.dma_start(q_raw[h][:], q_rows[:, :, h * R // 2 : (h + 1) * R // 2])
+        for j in range(2):
+            nc.sync.dma_start(v_pool[j][:], v_rows[:, j, :])
+        nc.sync.dma_start(do_raw[:], doT[0].rearrange("(p j) r -> p j r", j=PACK))
+        nc.sync.dma_start(v_pool_hi[:, 0, :], v_rows[:, 2, :])
+        nc.sync.dma_start(v_pool_hi[:, 1, :], v_rows[:, 3, :])
+        nc.sync.dma_start(qm_raw[:], qm[0].rearrange("(p t) d -> p t d", t=PACK))
+
+        ident = sb("ident", [P, P], F32)
+        make_identity(nc, ident[:])
+
+        k_g = sb("k_g", [P, PACK, N], F32)
+        kt_bf = []
+        kt_mx = mx_tiles("kt")
+
+        def turn_keys(j):
+            kt_bf.append(sb("kt_bf%d" % j, [P, P * PACK], BF16, "q_raw1" if j == PACK - 1 else None))
+            turned = bank("turn")
+            for t in range(PACK):
+                nc.tensor.transpose(turned[:, P * t : P * (t + 1)], k_g[:, j, t::PACK], ident[:])
+            nc.scalar.copy(
+                kt_bf[j][:].rearrange("m (p t) -> m p t", t=PACK),
+                turned[:].rearrange("m (t p) -> m p t", t=PACK),
+            )
+
+        for j in range(2):
+            nc.vector.tensor_copy(k_g[:, j, :], k_pool[j][:].indirect(offsets[:]))
+            turn_keys(j)
+
+        ts_g = sb("ts_g", [P, N], F32)
+        nc.vector.tensor_copy(ts_g[:], ts_pool[:].indirect(offsets[:]))
+        turned = bank("turn")
+        for s in range(PACK):
+            nc.tensor.transpose(turned[:, P * s : P * (s + 1)], ts_g[:, P * s : P * (s + 1)], ident[:])
+        ts_col = sb("ts_col", [P, PACK], F32)
+        nc.scalar.copy(ts_col[:], turned[:, 0::P])
+        turned = bank("turn")
+        for s in range(PACK):
+            nc.tensor.transpose(turned[:, P * s : P * (s + 1)], ts_col[:, s : s + 1].to_broadcast([P, P]), ident[:])
+        ts_row = sb("ts_row", [P, N], F32)
+        nc.scalar.copy(ts_row[:], turned[:])
+        neg_lse = sb("neg_lse", [P, PACK], F32)
+        nc.vector.tensor_scalar(neg_lse[:], lse_c[:], -1.0, None, ALU.mult)
+
+        for j in range(2, PACK):
+            nc.vector.tensor_copy(k_g[:, j, :], k_pool[j][:].indirect(offsets[:]))
+            if j < PACK - 1:
+                turn_keys(j)
+        k_bf = sb("k_bf", [P, N * PACK], BF16)
+        k_mx = mx_tiles("k")
+        nc.vector.tensor_copy(*interleave_views(k_bf, k_g, 0, N))
+        quantize(k_mx, E4, k_bf, 0, N)
+
+        q_bf = sb("q_bf", [P, R * PACK], BF16, "k_pool3")
+        q_mx = mx_tiles("q")
+        for h in range(2):
+            nc.scalar.copy(*query_views(q_bf, q_raw[h][:], h * P // 2, (h + 1) * P // 2))
+        quantize(q_mx, E4, q_bf, 0, R)
+        turn_keys(PACK - 1)
+
+        a_banks = [bank("turn") for t in range(PACK)]
+        a_sb = sb("a_sb", [P, PACK, R], F32)
+        scores = [bank("mm") for s in range(PACK)]
+        for s in range(PACK):
+            matmul(scores[s], k_mx, E4, s, q_mx, E4)
+        for s in range(PACK):
+            nc.scalar.activation(a_sb[:, s, :], scores[s][:], ACT.Copy, scale=ts_col[:, s : s + 1])
+            for t in range(PACK):
+                nc.tensor.transpose(a_banks[t][:, P * s : P * (s + 1)], a_sb[:, s, P * t : P * (t + 1)], ident[:])
+        p_sb = [sb("p_sb%d" % t, [P, N], F32) for t in range(PACK)]
+        for t in range(PACK):
+            nc.scalar.activation(p_sb[t][:], a_banks[t][:], ACT.Exp, bias=neg_lse[:, t : t + 1])
+
+        v_g = sb("v_g", [P, 2, N], F32, "k_pool3")
+        for j in range(2):
+            nc.vector.tensor_copy(v_g[:, j, :], v_pool[j][:].indirect(offsets[:]))
+        w_sb = [sb("w_sb%d" % t, [P, N], F32) for t in range(PACK)]
+
+        def weight(t):
+            nc.vector.scalar_tensor_tensor(
+                w_sb[t][:], p_sb[t][:], rw_c[:, t : t + 1], ts_row[:], ALU.mult, ALU.mult
+            )
+
+        for t in range(PACK):
+            weight(t)
+        do_bf = sb("do_bf", [P, R * PACK], BF16, "a_sb")
+        do_mx = mx_tiles("do")
+        nc.scalar.copy(*query_views(do_bf, do_raw[:], 0, P))
+        v_bf = sb("v_bf", [P, N * PACK], BF16, "p_sb3")
+        v_mx = mx_tiles("v")
+        v_view = v_bf[:].rearrange("p (i j) -> p i j", j=PACK)
+        nc.scalar.copy(v_view[:, :, 0:2], v_g[:].rearrange("p j i -> p i j"))
+        nc.vector.tensor_copy(v_view[:, :, 2], v_pool_hi[:, 0, :].indirect(offsets[:]))
+        quantize(do_mx, E5, do_bf, 0, R)
+        for h in range(2):
+            nc.vector.tensor_copy(
+                v_view[:, 256 * h : 256 * (h + 1), 3], v_pool_hi[:, 1, :].indirect(offsets[:, 16 * h : 16 * (h + 1)])
+            )
+        for h in range(2):
+            quantize(v_mx, E4, v_bf, 256 * h, 256 * (h + 1))
+        ds_bf = sb("ds_bf", [P, PACK, N], BF16)
+        for t in range(PACK):
+            dp = bank("mm")
+            matmul(dp, do_mx, E5, t, v_mx, E4)
+            nc.vector.scalar_tensor_tensor(
+                ds_bf[:, t, :], dp[:], delta_c[:, t : t + 1], w_sb[t][:], ALU.subtract, ALU.mult
+            )
+
+        qm_bf = sb("qm_bf", [P, D * PACK], BF16, "do_raw")
+        qm_mx = mx_tiles("qm", "w_sb0")
+        nc.scalar.copy(*interleave_views(qm_bf, qm_raw, 0, P))
+
+        dsr_bf = sb("dsr_bf", [P, N * PACK], BF16)
+        dsr_mx = mx_tiles("dsr")
+        nc.scalar.copy(*interleave_views(dsr_bf, ds_bf, DS_SPLIT, N))
+        nc.vector.tensor_copy(*interleave_views(dsr_bf, ds_bf, 0, DS_SPLIT))
+        quantize(qm_mx, E4, qm_bf, 0, P)
+        quantize(dsr_mx, E5, dsr_bf, 0, N)
+
+        windows = [sb("window%d" % b, [P, T], F32) for b in range(PACK)]
+        dk_sb = sb("dk_sb", [P, PACK, N], F32, "a_sb")
+
+        def key_gradient(b):
+            dk = bank("mm")
+            matmul(dk, qm_mx, E4, b, dsr_mx, E5)
+            nc.scalar.copy(dk_sb[:, b, :], dk[:])
+            nc.gpsimd.memset(windows[b][:], 0.0)
+            nc.vector.tensor_copy(windows[b][:].indirect(offsets[:]), dk_sb[:, b, :])
+            nc.sync.dma_start(out_1[P * b : P * (b + 1), :], windows[b][:])
+
+        key_gradient(0)
+
+        dss_bf = sb("dss_bf", [P, R * PACK], BF16)
+        dss_mx = mx_tiles("dss")
+        for t in range(PACK):
+            words = ds_bf[:, t, :].bitcast(F32)
+            turned = bank("turn")
+            for u in range(2):
+                nc.tensor.transpose(turned[:, P * u : P * (u + 1)], words[:, u::2], ident[:])
+            nc.scalar.copy(
+                dss_bf[:, 512 * t : 512 * (t + 1)].bitcast(F32).rearrange("p (m u) -> p m u", u=2),
+                turned[:, 0 : 2 * P].rearrange("p (u m) -> p m u", u=2),
+            )
+        for b in range(1, PACK):
+            nc.scalar.copy(*interleave_views(qm_bf, qm_raw, P * b, P * (b + 1)))
+        quantize(qm_mx, E4, qm_bf, P, 2 * P)
+        quantize(dss_mx, E5, dss_bf, 0, R)
+        quantize(qm_mx, E4, qm_bf, 2 * P, 4 * P)
+        for j in range(PACK):
+            nc.vector.quantize_mx(
+                out=kt_mx[0][:, P * j : P * (j + 1)].bitcast(E4), scales=kt_mx[1][:, P * j : P * (j + 1)], in_=kt_bf[j][:]
+            )
+        for b in range(1, PACK):
+            key_gradient(b)
+
+        gq_sb = sb("gq_sb", [P, PACK, D], F32, "k_pool0")
+        gq_rows = out_0[0].rearrange("(m t) d -> m t d", t=PACK)
+        for t in range(PACK):
+            gq = bank("turn")
+            matmul(gq, dss_mx, E5, t, kt_mx, E4)
+            nc.scalar.copy(
+                gq_sb[:, t, :].rearrange("m (p j) -> m p j", j=PACK),
+                gq[:].rearrange("m (j p) -> m p j", j=PACK),
+            )
+            nc.sync.dma_start(gq_rows[:, t, :], gq_sb[:, t, :])

@@ -18,6 +18,7 @@ ALU = mybir.AluOpType
 
 P = 128
 PACK = 4
+WINDOWS = 3
 DS_SPLIT = 352
 
 
@@ -74,8 +75,10 @@ def tile_attend_gat_lse_qk_ts_kernel(
         do_raw = sb("do_raw", [P, PACK, R], F32)
         qm_raw = sb("qm_raw", [P, PACK, D], F32)
         ts_pool = sb("ts_pool", [P, T], F32)
-        nc.vector.memset(ts_pool[:, 0 : T // 2], 0.0)
-        nc.gpsimd.memset(ts_pool[:, T // 2 : T], 0.0)
+        nc.vector.memset(ts_pool[:], 0.0)
+        windows = [sb("window%d" % b, [P, T], F32) for b in range(WINDOWS)]
+        for window in windows:
+            nc.vector.memset(window[:], 0.0)
         nc.sync.dma_start(ts_pool[0:1, :], ts[0:1, :])
         lse_c = sb("lse_c", [P, PACK], F32)
         delta_c = sb("delta_c", [P, PACK], F32)
@@ -211,16 +214,15 @@ def tile_attend_gat_lse_qk_ts_kernel(
         quantize(qm_mx, E4, qm_bf, 0, P)
         quantize(dsr_mx, E5, dsr_bf, 0, N)
 
-        windows = [sb("window%d" % b, [P, T], F32) for b in range(PACK)]
         dk_sb = sb("dk_sb", [P, PACK, N], F32, "a_sb")
 
         def key_gradient(b):
             dk = bank("mm")
             matmul(dk, qm_mx, E4, b, dsr_mx, E5)
             nc.scalar.copy(dk_sb[:, b, :], dk[:])
-            nc.gpsimd.memset(windows[b][:], 0.0)
-            nc.vector.tensor_copy(windows[b][:].indirect(offsets[:]), dk_sb[:, b, :])
-            nc.sync.dma_start(out_1[P * b : P * (b + 1), :], windows[b][:])
+            window = windows[b % WINDOWS]
+            nc.vector.tensor_copy(window[:].indirect(offsets[:]), dk_sb[:, b, :])
+            nc.sync.dma_start(out_1[P * b : P * (b + 1), :], window[:])
 
         key_gradient(0)
 

@@ -19,6 +19,7 @@ ALU = mybir.AluOpType
 P = 128
 PACK = 4
 WINDOWS = 3
+DO_SPLIT = 88
 DS_SPLIT = 352
 
 
@@ -69,16 +70,14 @@ def tile_attend_gat_lse_qk_ts_kernel(
         k_rows = kT.rearrange("(p j) t -> p j t", j=PACK)
         v_rows = vT.rearrange("(p j) t -> p j t", j=PACK)
         k_pool = [sb("k_pool%d" % j, [P, T], F32) for j in range(PACK)]
-        v_pool = [sb("v_pool%d" % j, [P, T], F32) for j in range(2)]
-        v_pool_hi = sb("v_pool_hi", [P, 2, T], F32)
+        v_pool = [sb("v_pool%d" % j, [P, T], F32) for j in range(PACK)]
         q_raw = [sb("q_raw%d" % h, [P, PACK, R // 2], F32) for h in range(2)]
         do_raw = sb("do_raw", [P, PACK, R], F32)
         qm_raw = sb("qm_raw", [P, PACK, D], F32)
         ts_pool = sb("ts_pool", [P, T], F32)
         nc.vector.memset(ts_pool[:], 0.0)
         windows = [sb("window%d" % b, [P, T], F32) for b in range(WINDOWS)]
-        for window in windows:
-            nc.vector.memset(window[:], 0.0)
+        nc.vector.memset(windows[0][:], 0.0)
         nc.sync.dma_start(ts_pool[0:1, :], ts[0:1, :])
         lse_c = sb("lse_c", [P, PACK], F32)
         delta_c = sb("delta_c", [P, PACK], F32)
@@ -99,12 +98,14 @@ def tile_attend_gat_lse_qk_ts_kernel(
         for j in range(2):
             nc.sync.dma_start(v_pool[j][:], v_rows[:, j, :])
         nc.sync.dma_start(do_raw[:], doT[0].rearrange("(p j) r -> p j r", j=PACK))
-        nc.sync.dma_start(v_pool_hi[:, 0, :], v_rows[:, 2, :])
-        nc.sync.dma_start(v_pool_hi[:, 1, :], v_rows[:, 3, :])
+        for j in range(2, PACK):
+            nc.sync.dma_start(v_pool[j][:], v_rows[:, j, :])
         nc.sync.dma_start(qm_raw[:], qm[0].rearrange("(p t) d -> p t d", t=PACK))
 
         ident = sb("ident", [P, P], F32)
         make_identity(nc, ident[:])
+        for window in windows[1:]:
+            nc.gpsimd.memset(window[:], 0.0)
 
         k_g = sb("k_g", [P, PACK, N], F32)
         kt_bf = []
@@ -123,6 +124,10 @@ def tile_attend_gat_lse_qk_ts_kernel(
         for j in range(2):
             nc.vector.tensor_copy(k_g[:, j, :], k_pool[j][:].indirect(offsets[:]))
             turn_keys(j)
+
+        k_bf = sb("k_bf", [P, N * PACK], BF16)
+        k_view = k_bf[:].rearrange("p (i j) -> p i j", j=PACK)
+        nc.scalar.copy(k_view[:, :, 0:2], k_g[:, 0:2, :].rearrange("p j i -> p i j"))
 
         ts_g = sb("ts_g", [P, N], F32)
         nc.vector.tensor_copy(ts_g[:], ts_pool[:].indirect(offsets[:]))
@@ -143,32 +148,51 @@ def tile_attend_gat_lse_qk_ts_kernel(
             nc.vector.tensor_copy(k_g[:, j, :], k_pool[j][:].indirect(offsets[:]))
             if j < PACK - 1:
                 turn_keys(j)
-        k_bf = sb("k_bf", [P, N * PACK], BF16)
         k_mx = mx_tiles("k")
-        nc.vector.tensor_copy(*interleave_views(k_bf, k_g, 0, N))
+        nc.vector.tensor_copy(k_view[:, :, 2:4], k_g[:, 2:4, :].rearrange("p j i -> p i j"))
         quantize(k_mx, E4, k_bf, 0, N)
 
         q_bf = sb("q_bf", [P, R * PACK], BF16, "k_pool3")
         q_mx = mx_tiles("q")
-        for h in range(2):
-            nc.scalar.copy(*query_views(q_bf, q_raw[h][:], h * P // 2, (h + 1) * P // 2))
+        nc.scalar.copy(*query_views(q_bf, q_raw[0][:], 0, 64))
+        nc.scalar.copy(*query_views(q_bf, q_raw[1][:, :, 0:128], 64, 96))
+        nc.vector.tensor_copy(*query_views(q_bf, q_raw[1][:, :, 128:256], 96, 128))
         quantize(q_mx, E4, q_bf, 0, R)
         turn_keys(PACK - 1)
 
+        a_first = sb("a_first", [P, N], F32)
+        v_g = sb("v_g", [P, PACK, N], F32, "k_pool3")
+        a_direct = [a_first[:], v_g[:, 1, :]]
+        a_sb = sb("a_sb", [P, PACK, 256], F32)
         a_banks = [bank("turn") for t in range(PACK)]
-        a_sb = sb("a_sb", [P, PACK, R], F32)
+        for t in range(2):
+            matmul(a_banks[t], q_mx, E4, t, k_mx, E4)
         scores = [bank("mm") for s in range(PACK)]
         for s in range(PACK):
-            matmul(scores[s], k_mx, E4, s, q_mx, E4)
+            cols = slice(P * s, P * (s + 1))
+            nc.tensor.matmul_mx(
+                out=scores[s][:, 0:256],
+                lhsT=k_mx[0][:, cols].bitcast(E4),
+                lhsT_scale=k_mx[1][:, cols],
+                rhs=q_mx[0][:, 256:512].bitcast(E4),
+                rhs_scale=q_mx[1][:, 256:512],
+                start=True,
+                stop=True,
+            )
+        for t in range(2):
+            nc.vector.tensor_tensor(a_direct[t], a_banks[t][:], ts_row[:], ALU.mult)
         for s in range(PACK):
-            nc.scalar.activation(a_sb[:, s, :], scores[s][:], ACT.Copy, scale=ts_col[:, s : s + 1])
-            for t in range(PACK):
-                nc.tensor.transpose(a_banks[t][:, P * s : P * (s + 1)], a_sb[:, s, P * t : P * (t + 1)], ident[:])
+            nc.scalar.activation(a_sb[:, s, :], scores[s][:, 0:256], ACT.Copy, scale=ts_col[:, s : s + 1])
+        for t in range(2, PACK):
+            for s in range(PACK):
+                nc.tensor.transpose(
+                    a_banks[t][:, P * s : P * (s + 1)], a_sb[:, s, P * (t - 2) : P * (t - 1)], ident[:]
+                )
         p_sb = [sb("p_sb%d" % t, [P, N], F32) for t in range(PACK)]
         for t in range(PACK):
-            nc.scalar.activation(p_sb[t][:], a_banks[t][:], ACT.Exp, bias=neg_lse[:, t : t + 1])
+            src = a_direct[t] if t < 2 else a_banks[t][:]
+            nc.scalar.activation(p_sb[t][:], src, ACT.Exp, bias=neg_lse[:, t : t + 1])
 
-        v_g = sb("v_g", [P, 2, N], F32, "k_pool3")
         for j in range(2):
             nc.vector.tensor_copy(v_g[:, j, :], v_pool[j][:].indirect(offsets[:]))
         w_sb = [sb("w_sb%d" % t, [P, N], F32) for t in range(PACK)]
@@ -180,21 +204,26 @@ def tile_attend_gat_lse_qk_ts_kernel(
 
         for t in range(PACK):
             weight(t)
-        do_bf = sb("do_bf", [P, R * PACK], BF16, "a_sb")
-        do_mx = mx_tiles("do")
-        nc.scalar.copy(*query_views(do_bf, do_raw[:], 0, P))
-        v_bf = sb("v_bf", [P, N * PACK], BF16, "p_sb3")
+        do_bf = sb("do_bf", [P, R * PACK], BF16, "neg_lse")
+        nc.scalar.copy(*query_views(do_bf, do_raw[:, :, 0 : PACK * DO_SPLIT], 0, DO_SPLIT))
+        v_bf = sb("v_bf", [P, N * PACK], BF16, "a_sb")
         v_mx = mx_tiles("v")
         v_view = v_bf[:].rearrange("p (i j) -> p i j", j=PACK)
-        nc.scalar.copy(v_view[:, :, 0:2], v_g[:].rearrange("p j i -> p i j"))
-        nc.vector.tensor_copy(v_view[:, :, 2], v_pool_hi[:, 0, :].indirect(offsets[:]))
+        nc.scalar.copy(v_view[:, :, 0:2], v_g[:, 0:2, :].rearrange("p j i -> p i j"))
+        nc.vector.tensor_copy(v_g[:, 2, :], v_pool[2][:].indirect(offsets[:]))
+        nc.vector.tensor_copy(*query_views(do_bf, do_raw[:, :, PACK * DO_SPLIT : R], DO_SPLIT, P))
+        for h in range(2):
+            half = slice(256 * h, 256 * (h + 1))
+            nc.vector.tensor_copy(v_g[:, 3, half], v_pool[3][:].indirect(offsets[:, 16 * h : 16 * (h + 1)]))
+            nc.scalar.copy(v_view[:, half, 2:4], v_g[:, 2:4, half].rearrange("p j i -> p i j"))
+        do_mx = mx_tiles("do", "v_pool3")
         quantize(do_mx, E5, do_bf, 0, R)
         for h in range(2):
-            nc.vector.tensor_copy(
-                v_view[:, 256 * h : 256 * (h + 1), 3], v_pool_hi[:, 1, :].indirect(offsets[:, 16 * h : 16 * (h + 1)])
-            )
-        for h in range(2):
             quantize(v_mx, E4, v_bf, 256 * h, 256 * (h + 1))
+        qm_bf = sb("qm_bf", [P, D * PACK], BF16, "k_pool3")
+        qm_mx = mx_tiles("qm", "a_sb")
+        nc.scalar.copy(*interleave_views(qm_bf, qm_raw, 0, P))
+        quantize(qm_mx, E4, qm_bf, 0, P)
         ds_bf = sb("ds_bf", [P, PACK, N], BF16)
         for t in range(PACK):
             dp = bank("mm")
@@ -203,25 +232,29 @@ def tile_attend_gat_lse_qk_ts_kernel(
                 ds_bf[:, t, :], dp[:], delta_c[:, t : t + 1], w_sb[t][:], ALU.subtract, ALU.mult
             )
 
-        qm_bf = sb("qm_bf", [P, D * PACK], BF16, "do_raw")
-        qm_mx = mx_tiles("qm", "w_sb0")
-        nc.scalar.copy(*interleave_views(qm_bf, qm_raw, 0, P))
-
         dsr_bf = sb("dsr_bf", [P, N * PACK], BF16)
         dsr_mx = mx_tiles("dsr")
         nc.scalar.copy(*interleave_views(dsr_bf, ds_bf, DS_SPLIT, N))
-        nc.vector.tensor_copy(*interleave_views(dsr_bf, ds_bf, 0, DS_SPLIT))
-        quantize(qm_mx, E4, qm_bf, 0, P)
-        quantize(dsr_mx, E5, dsr_bf, 0, N)
+        nc.vector.tensor_copy(*interleave_views(dsr_bf, ds_bf, 0, 256))
+        nc.vector.tensor_copy(*interleave_views(dsr_bf, ds_bf, 256, DS_SPLIT))
+        quantize(dsr_mx, E5, dsr_bf, 0, 256)
+        quantize(dsr_mx, E5, dsr_bf, 256, N)
 
-        dk_sb = sb("dk_sb", [P, PACK, N], F32, "a_sb")
+        dk_sb = sb("dk_sb", [P, PACK, N], F32, "k_pool1")
 
         def key_gradient(b):
             dk = bank("mm")
             matmul(dk, qm_mx, E4, b, dsr_mx, E5)
-            nc.scalar.copy(dk_sb[:, b, :], dk[:])
             window = windows[b % WINDOWS]
-            nc.vector.tensor_copy(window[:].indirect(offsets[:]), dk_sb[:, b, :])
+            pieces = 2 if b == 0 else 1
+            width = N // pieces
+            for h in range(pieces):
+                nc.scalar.copy(dk_sb[:, b, width * h : width * (h + 1)], dk[:, width * h : width * (h + 1)])
+            for h in range(pieces):
+                nc.vector.tensor_copy(
+                    window[:].indirect(offsets[:, width // 16 * h : width // 16 * (h + 1)]),
+                    dk_sb[:, b, width * h : width * (h + 1)],
+                )
             nc.sync.dma_start(out_1[P * b : P * (b + 1), :], window[:])
 
         key_gradient(0)
@@ -258,4 +291,4 @@ def tile_attend_gat_lse_qk_ts_kernel(
                 gq_sb[:, t, :].rearrange("m (p j) -> m p j", j=PACK),
                 gq[:].rearrange("m (j p) -> m p j", j=PACK),
             )
-            nc.sync.dma_start(gq_rows[:, t, :], gq_sb[:, t, :])
+            nc.scalar.dma_start(gq_rows[:, t, :], gq_sb[:, t, :])

@@ -11,14 +11,21 @@ BF16 = mybir.dt.bfloat16
 U32 = mybir.dt.uint32
 U16 = mybir.dt.uint16
 U8 = mybir.dt.uint8
-E4 = mybir.dt.float8_e4m3fn_x4
-E5 = mybir.dt.float8_e5m2_x4
+E4M3 = mybir.dt.float8_e4m3fn_x4
+E5M2 = mybir.dt.float8_e5m2_x4
 ACT = mybir.ActivationFunctionType
 ALU = mybir.AluOpType
 
 P = 128
 PACK = 4
+WIDTH = 512
+HALF = WIDTH // 2
+BAND = 16
+RUN = 4
+BANKS_PER_TAG = 4
 WINDOWS = 3
+DIRECT = 2
+Q_SPLIT = 96
 DO_SPLIT = 88
 DS_SPLIT = 352
 
@@ -29,49 +36,57 @@ def tile_attend_gat_lse_qk_ts_kernel(
     nc = tc.nc
     with ExitStack() as ctx:
         keep = ctx.enter_context(tc.tile_pool(name="keep", bufs=1))
-        psum = ctx.enter_context(tc.psum_pool(name="psum", bufs=4))
+        psum = ctx.enter_context(tc.psum_pool(name="psum", bufs=BANKS_PER_TAG))
 
-        def sb(name, shape, dtype, tag=None):
-            return keep.tile(shape, dtype, name=name, tag=tag or name, align_bytes=64)
+        def sb(name, shape, dtype, reuse=None):
+            return keep.tile(shape, dtype, name=name, tag=reuse or name, align_bytes=64)
 
         def bank(tag):
-            return psum.tile([P, 512], F32, name=tag, tag=tag)
+            return psum.tile([P, WIDTH], F32, name=tag, tag=tag)
 
-        def mx_tiles(name, tag=None):
-            return sb(name + "_codes", [P, 512], U32, tag), sb(name + "_scales", [P, 512], U8)
+        def mx_tiles(name, reuse=None):
+            return sb(name + "_codes", [P, WIDTH], U32, reuse), sb(name + "_scales", [P, WIDTH], U8)
 
-        def quantize(mx, fmt, src, c0, c1):
-            nc.vector.quantize_mx(
-                out=mx[0][:, c0:c1].bitcast(fmt), scales=mx[1][:, c0:c1], in_=src[:, PACK * c0 : PACK * c1]
-            )
+        def quantize(mx, fmt, c0, c1, values):
+            nc.vector.quantize_mx(out=mx[0][:, c0:c1].bitcast(fmt), scales=mx[1][:, c0:c1], in_=values)
 
-        def matmul(out, stat, stat_fmt, block, mov, mov_fmt):
+        def laid(tile, c0, c1):
+            return tile[:, PACK * c0 : PACK * c1]
+
+        def matmul(out, stationary, stationary_fmt, block, moving, moving_fmt, c0=0):
             cols = slice(P * block, P * (block + 1))
             nc.tensor.matmul_mx(
-                out=out[:],
-                lhsT=stat[0][:, cols].bitcast(stat_fmt),
-                lhsT_scale=stat[1][:, cols],
-                rhs=mov[0][:].bitcast(mov_fmt),
-                rhs_scale=mov[1][:],
+                out=out,
+                lhsT=stationary[0][:, cols].bitcast(stationary_fmt),
+                lhsT_scale=stationary[1][:, cols],
+                rhs=moving[0][:, c0:WIDTH].bitcast(moving_fmt),
+                rhs_scale=moving[1][:, c0:WIDTH],
                 start=True,
                 stop=True,
             )
 
-        def interleave_views(dst, src, c0, c1):
-            out = dst[:, PACK * c0 : PACK * c1].rearrange("p (c i j) -> p c j i", i=4, j=PACK)
-            return out, src[:, :, c0:c1].rearrange("p j (c i) -> p c j i", i=4)
+        def gather(out, window, c0=0, c1=N):
+            nc.vector.tensor_copy(out, window[:].indirect(offsets[:, c0 // BAND : c1 // BAND]))
 
-        def query_views(dst, src, m0, m1):
+        def interleave_views(dst, planes, c0, c1):
+            out = laid(dst, c0, c1).rearrange("p (c i j) -> p c j i", i=RUN, j=PACK)
+            return out, planes[:, :, c0:c1].rearrange("p j (c i) -> p c j i", i=RUN)
+
+        def pair_views(dst, planes, j0, cols):
+            out = dst[:].rearrange("p (c j) -> p c j", j=PACK)[:, cols, j0 : j0 + 2]
+            return out, planes[:, j0 : j0 + 2, cols].rearrange("p j c -> p c j")
+
+        def query_views(dst, planes, m0, m1):
             out = dst[:].rearrange("p (t m j) -> p m j t", t=PACK, j=PACK)[:, m0:m1]
-            return out, src.rearrange("p j (m t) -> p m j t", t=PACK)
+            return out, planes.rearrange("p j (m t) -> p m j t", t=PACK)
 
-        offsets = keep.tile([P, N // 16], U16, name="offsets")
+        offsets = keep.tile([P, N // BAND], U16, name="offsets")
         nc.sync.dma_start(offsets[:], offs)
         k_rows = kT.rearrange("(p j) t -> p j t", j=PACK)
         v_rows = vT.rearrange("(p j) t -> p j t", j=PACK)
         k_pool = [sb("k_pool%d" % j, [P, T], F32) for j in range(PACK)]
         v_pool = [sb("v_pool%d" % j, [P, T], F32) for j in range(PACK)]
-        q_raw = [sb("q_raw%d" % h, [P, PACK, R // 2], F32) for h in range(2)]
+        q_raw = [sb("q_raw%d" % h, [P, PACK, HALF], F32) for h in range(2)]
         do_raw = sb("do_raw", [P, PACK, R], F32)
         qm_raw = sb("qm_raw", [P, PACK, D], F32)
         ts_pool = sb("ts_pool", [P, T], F32)
@@ -82,19 +97,18 @@ def tile_attend_gat_lse_qk_ts_kernel(
         lse_c = sb("lse_c", [P, PACK], F32)
         delta_c = sb("delta_c", [P, PACK], F32)
         rw_c = sb("rw_c", [P, PACK], F32)
-        for h in range(2):
-            half = slice(h * T // 2, (h + 1) * T // 2)
-            nc.sync.dma_start(k_pool[0][:, half], k_rows[:, 0, half])
-        for tile, src in ((lse_c, lse), (delta_c, delta), (rw_c, rw)):
-            nc.sync.dma_start(tile[:], src[0].rearrange("(p t) o -> p (t o)", t=PACK))
-        for h in range(2):
-            half = slice(h * T // 2, (h + 1) * T // 2)
-            nc.sync.dma_start(k_pool[1][:, half], k_rows[:, 1, half])
+        token_halves = [slice(0, T // 2), slice(T // 2, T)]
+        for tokens in token_halves:
+            nc.sync.dma_start(k_pool[0][:, tokens], k_rows[:, 0, tokens])
+        for columns, vector in ((lse_c, lse), (delta_c, delta), (rw_c, rw)):
+            nc.sync.dma_start(columns[:], vector[0].rearrange("(p t) o -> p (t o)", t=PACK))
+        for tokens in token_halves:
+            nc.sync.dma_start(k_pool[1][:, tokens], k_rows[:, 1, tokens])
         for j in range(2, PACK):
             nc.sync.dma_start(k_pool[j][:], k_rows[:, j, :])
         q_rows = qT[0].rearrange("(p j) r -> p j r", j=PACK)
         for h in range(2):
-            nc.sync.dma_start(q_raw[h][:], q_rows[:, :, h * R // 2 : (h + 1) * R // 2])
+            nc.sync.dma_start(q_raw[h][:], q_rows[:, :, HALF * h : HALF * (h + 1)])
         for j in range(2):
             nc.sync.dma_start(v_pool[j][:], v_rows[:, j, :])
         nc.sync.dma_start(do_raw[:], doT[0].rearrange("(p j) r -> p j r", j=PACK))
@@ -108,29 +122,27 @@ def tile_attend_gat_lse_qk_ts_kernel(
             nc.gpsimd.memset(window[:], 0.0)
 
         k_g = sb("k_g", [P, PACK, N], F32)
-        kt_bf = []
+        kt_bf = [sb("kt_bf0", [P, 2, WIDTH], BF16)]
         kt_mx = mx_tiles("kt")
 
         def turn_keys(j):
-            kt_bf.append(sb("kt_bf%d" % j, [P, P * PACK], BF16, "q_raw1" if j == PACK - 1 else None))
             turned = bank("turn")
             for t in range(PACK):
                 nc.tensor.transpose(turned[:, P * t : P * (t + 1)], k_g[:, j, t::PACK], ident[:])
             nc.scalar.copy(
-                kt_bf[j][:].rearrange("m (p t) -> m p t", t=PACK),
+                kt_bf[j // 2][:, j % 2, :].rearrange("m (p t) -> m p t", t=PACK),
                 turned[:].rearrange("m (t p) -> m p t", t=PACK),
             )
 
         for j in range(2):
-            nc.vector.tensor_copy(k_g[:, j, :], k_pool[j][:].indirect(offsets[:]))
+            gather(k_g[:, j, :], k_pool[j])
             turn_keys(j)
-
+        all_slots = slice(0, N)
         k_bf = sb("k_bf", [P, N * PACK], BF16)
-        k_view = k_bf[:].rearrange("p (i j) -> p i j", j=PACK)
-        nc.scalar.copy(k_view[:, :, 0:2], k_g[:, 0:2, :].rearrange("p j i -> p i j"))
+        nc.vector.tensor_copy(*pair_views(k_bf, k_g, 0, all_slots))
 
         ts_g = sb("ts_g", [P, N], F32)
-        nc.vector.tensor_copy(ts_g[:], ts_pool[:].indirect(offsets[:]))
+        gather(ts_g[:], ts_pool)
         turned = bank("turn")
         for s in range(PACK):
             nc.tensor.transpose(turned[:, P * s : P * (s + 1)], ts_g[:, P * s : P * (s + 1)], ident[:])
@@ -145,89 +157,76 @@ def tile_attend_gat_lse_qk_ts_kernel(
         nc.vector.tensor_scalar(neg_lse[:], lse_c[:], -1.0, None, ALU.mult)
 
         for j in range(2, PACK):
-            nc.vector.tensor_copy(k_g[:, j, :], k_pool[j][:].indirect(offsets[:]))
-            if j < PACK - 1:
-                turn_keys(j)
+            gather(k_g[:, j, :], k_pool[j])
         k_mx = mx_tiles("k")
-        nc.vector.tensor_copy(k_view[:, :, 2:4], k_g[:, 2:4, :].rearrange("p j i -> p i j"))
-        quantize(k_mx, E4, k_bf, 0, N)
+        nc.vector.tensor_copy(*pair_views(k_bf, k_g, 2, all_slots))
+        quantize(k_mx, E4M3, 0, N, k_bf[:])
 
         q_bf = sb("q_bf", [P, R * PACK], BF16, "k_pool3")
         q_mx = mx_tiles("q")
-        nc.scalar.copy(*query_views(q_bf, q_raw[0][:], 0, 64))
-        nc.scalar.copy(*query_views(q_bf, q_raw[1][:, :, 0:128], 64, 96))
-        nc.vector.tensor_copy(*query_views(q_bf, q_raw[1][:, :, 128:256], 96, 128))
-        quantize(q_mx, E4, q_bf, 0, R)
-        turn_keys(PACK - 1)
+        q_cut = PACK * Q_SPLIT - HALF
+        nc.scalar.copy(*query_views(q_bf, q_raw[0][:], 0, P // 2))
+        nc.scalar.copy(*query_views(q_bf, q_raw[1][:, :, 0:q_cut], P // 2, Q_SPLIT))
+        nc.vector.tensor_copy(*query_views(q_bf, q_raw[1][:, :, q_cut:HALF], Q_SPLIT, P))
+        quantize(q_mx, E4M3, 0, R, q_bf[:])
+        kt_bf.append(sb("kt_bf1", [P, 2, WIDTH], BF16, "q_raw1"))
+        for j in range(2, PACK):
+            turn_keys(j)
 
-        a_first = sb("a_first", [P, N], F32)
+        a_direct = sb("a_direct", [P, DIRECT, N], F32)
         v_g = sb("v_g", [P, PACK, N], F32, "k_pool3")
-        a_direct = [a_first[:], v_g[:, 1, :]]
-        a_sb = sb("a_sb", [P, PACK, 256], F32)
+        a_slots = sb("a_slots", [P, PACK, HALF], F32)
         a_banks = [bank("turn") for t in range(PACK)]
-        for t in range(2):
-            matmul(a_banks[t], q_mx, E4, t, k_mx, E4)
-        scores = [bank("mm") for s in range(PACK)]
+        for t in range(DIRECT):
+            matmul(a_banks[t][:], q_mx, E4M3, t, k_mx, E4M3)
+        slot_banks = [bank("mm") for s in range(PACK)]
         for s in range(PACK):
-            cols = slice(P * s, P * (s + 1))
-            nc.tensor.matmul_mx(
-                out=scores[s][:, 0:256],
-                lhsT=k_mx[0][:, cols].bitcast(E4),
-                lhsT_scale=k_mx[1][:, cols],
-                rhs=q_mx[0][:, 256:512].bitcast(E4),
-                rhs_scale=q_mx[1][:, 256:512],
-                start=True,
-                stop=True,
-            )
-        for t in range(2):
-            nc.vector.tensor_tensor(a_direct[t], a_banks[t][:], ts_row[:], ALU.mult)
+            matmul(slot_banks[s][:, 0:HALF], k_mx, E4M3, s, q_mx, E4M3, P * DIRECT)
+        for t in range(DIRECT):
+            nc.vector.tensor_tensor(a_direct[:, t, :], a_banks[t][:], ts_row[:], ALU.mult)
         for s in range(PACK):
-            nc.scalar.activation(a_sb[:, s, :], scores[s][:, 0:256], ACT.Copy, scale=ts_col[:, s : s + 1])
-        for t in range(2, PACK):
+            nc.scalar.activation(a_slots[:, s, :], slot_banks[s][:, 0:HALF], ACT.Copy, scale=ts_col[:, s : s + 1])
+        for t in range(DIRECT, PACK):
+            queries = slice(P * (t - DIRECT), P * (t - DIRECT + 1))
             for s in range(PACK):
-                nc.tensor.transpose(
-                    a_banks[t][:, P * s : P * (s + 1)], a_sb[:, s, P * (t - 2) : P * (t - 1)], ident[:]
-                )
+                nc.tensor.transpose(a_banks[t][:, P * s : P * (s + 1)], a_slots[:, s, queries], ident[:])
         p_sb = [sb("p_sb%d" % t, [P, N], F32) for t in range(PACK)]
         for t in range(PACK):
-            src = a_direct[t] if t < 2 else a_banks[t][:]
-            nc.scalar.activation(p_sb[t][:], src, ACT.Exp, bias=neg_lse[:, t : t + 1])
+            scaled = a_direct[:, t, :] if t < DIRECT else a_banks[t][:]
+            nc.scalar.activation(p_sb[t][:], scaled, ACT.Exp, bias=neg_lse[:, t : t + 1])
 
         for j in range(2):
-            nc.vector.tensor_copy(v_g[:, j, :], v_pool[j][:].indirect(offsets[:]))
+            gather(v_g[:, j, :], v_pool[j])
         w_sb = [sb("w_sb%d" % t, [P, N], F32) for t in range(PACK)]
-
-        def weight(t):
+        for t in range(PACK):
             nc.vector.scalar_tensor_tensor(
                 w_sb[t][:], p_sb[t][:], rw_c[:, t : t + 1], ts_row[:], ALU.mult, ALU.mult
             )
-
-        for t in range(PACK):
-            weight(t)
         do_bf = sb("do_bf", [P, R * PACK], BF16, "neg_lse")
         nc.scalar.copy(*query_views(do_bf, do_raw[:, :, 0 : PACK * DO_SPLIT], 0, DO_SPLIT))
-        v_bf = sb("v_bf", [P, N * PACK], BF16, "a_sb")
+        v_bf = sb("v_bf", [P, N * PACK], BF16, "a_slots")
         v_mx = mx_tiles("v")
-        v_view = v_bf[:].rearrange("p (i j) -> p i j", j=PACK)
-        nc.scalar.copy(v_view[:, :, 0:2], v_g[:, 0:2, :].rearrange("p j i -> p i j"))
-        nc.vector.tensor_copy(v_g[:, 2, :], v_pool[2][:].indirect(offsets[:]))
+        nc.scalar.copy(*pair_views(v_bf, v_g, 0, all_slots))
+        gather(v_g[:, 2, :], v_pool[2])
         nc.vector.tensor_copy(*query_views(do_bf, do_raw[:, :, PACK * DO_SPLIT : R], DO_SPLIT, P))
-        for h in range(2):
-            half = slice(256 * h, 256 * (h + 1))
-            nc.vector.tensor_copy(v_g[:, 3, half], v_pool[3][:].indirect(offsets[:, 16 * h : 16 * (h + 1)]))
-            nc.scalar.copy(v_view[:, half, 2:4], v_g[:, 2:4, half].rearrange("p j i -> p i j"))
+        for c0 in (0, HALF):
+            slots = slice(c0, c0 + HALF)
+            gather(v_g[:, 3, slots], v_pool[3], c0, c0 + HALF)
+            nc.scalar.copy(*pair_views(v_bf, v_g, 2, slots))
         do_mx = mx_tiles("do", "v_pool3")
-        quantize(do_mx, E5, do_bf, 0, R)
-        for h in range(2):
-            quantize(v_mx, E4, v_bf, 256 * h, 256 * (h + 1))
+        quantize(do_mx, E5M2, 0, R, do_bf[:])
+        for c0 in (0, HALF):
+            quantize(v_mx, E4M3, c0, c0 + HALF, laid(v_bf, c0, c0 + HALF))
+
         qm_bf = sb("qm_bf", [P, D * PACK], BF16, "k_pool3")
-        qm_mx = mx_tiles("qm", "a_sb")
+        qm_mx = mx_tiles("qm", "a_slots")
         nc.scalar.copy(*interleave_views(qm_bf, qm_raw, 0, P))
-        quantize(qm_mx, E4, qm_bf, 0, P)
+        quantize(qm_mx, E4M3, 0, P, laid(qm_bf, 0, P))
+
         ds_bf = sb("ds_bf", [P, PACK, N], BF16)
         for t in range(PACK):
             dp = bank("mm")
-            matmul(dp, do_mx, E5, t, v_mx, E4)
+            matmul(dp[:], do_mx, E5M2, t, v_mx, E4M3)
             nc.vector.scalar_tensor_tensor(
                 ds_bf[:, t, :], dp[:], delta_c[:, t : t + 1], w_sb[t][:], ALU.subtract, ALU.mult
             )
@@ -235,29 +234,26 @@ def tile_attend_gat_lse_qk_ts_kernel(
         dsr_bf = sb("dsr_bf", [P, N * PACK], BF16)
         dsr_mx = mx_tiles("dsr")
         nc.scalar.copy(*interleave_views(dsr_bf, ds_bf, DS_SPLIT, N))
-        nc.vector.tensor_copy(*interleave_views(dsr_bf, ds_bf, 0, 256))
-        nc.vector.tensor_copy(*interleave_views(dsr_bf, ds_bf, 256, DS_SPLIT))
-        quantize(dsr_mx, E5, dsr_bf, 0, 256)
-        quantize(dsr_mx, E5, dsr_bf, 256, N)
+        nc.vector.tensor_copy(*interleave_views(dsr_bf, ds_bf, 0, HALF))
+        nc.vector.tensor_copy(*interleave_views(dsr_bf, ds_bf, HALF, DS_SPLIT))
+        for c0 in (0, HALF):
+            quantize(dsr_mx, E5M2, c0, c0 + HALF, laid(dsr_bf, c0, c0 + HALF))
 
         dk_sb = sb("dk_sb", [P, PACK, N], F32, "k_pool1")
 
-        def key_gradient(b):
+        def key_gradient(b, width):
             dk = bank("mm")
-            matmul(dk, qm_mx, E4, b, dsr_mx, E5)
+            matmul(dk[:], qm_mx, E4M3, b, dsr_mx, E5M2)
             window = windows[b % WINDOWS]
-            pieces = 2 if b == 0 else 1
-            width = N // pieces
-            for h in range(pieces):
-                nc.scalar.copy(dk_sb[:, b, width * h : width * (h + 1)], dk[:, width * h : width * (h + 1)])
-            for h in range(pieces):
+            for c0 in range(0, N, width):
+                nc.scalar.copy(dk_sb[:, b, c0 : c0 + width], dk[:, c0 : c0 + width])
+            for c0 in range(0, N, width):
                 nc.vector.tensor_copy(
-                    window[:].indirect(offsets[:, width // 16 * h : width // 16 * (h + 1)]),
-                    dk_sb[:, b, width * h : width * (h + 1)],
+                    window[:].indirect(offsets[:, c0 // BAND : (c0 + width) // BAND]), dk_sb[:, b, c0 : c0 + width]
                 )
             nc.sync.dma_start(out_1[P * b : P * (b + 1), :], window[:])
 
-        key_gradient(0)
+        key_gradient(0, HALF)
 
         dss_bf = sb("dss_bf", [P, R * PACK], BF16)
         dss_mx = mx_tiles("dss")
@@ -267,26 +263,24 @@ def tile_attend_gat_lse_qk_ts_kernel(
             for u in range(2):
                 nc.tensor.transpose(turned[:, P * u : P * (u + 1)], words[:, u::2], ident[:])
             nc.scalar.copy(
-                dss_bf[:, 512 * t : 512 * (t + 1)].bitcast(F32).rearrange("p (m u) -> p m u", u=2),
+                laid(dss_bf, P * t, P * (t + 1)).bitcast(F32).rearrange("p (m u) -> p m u", u=2),
                 turned[:, 0 : 2 * P].rearrange("p (u m) -> p m u", u=2),
             )
         for b in range(1, PACK):
             nc.scalar.copy(*interleave_views(qm_bf, qm_raw, P * b, P * (b + 1)))
-        quantize(qm_mx, E4, qm_bf, P, 2 * P)
-        quantize(dss_mx, E5, dss_bf, 0, R)
-        quantize(qm_mx, E4, qm_bf, 2 * P, 4 * P)
-        for j in range(PACK):
-            nc.vector.quantize_mx(
-                out=kt_mx[0][:, P * j : P * (j + 1)].bitcast(E4), scales=kt_mx[1][:, P * j : P * (j + 1)], in_=kt_bf[j][:]
-            )
+        quantize(qm_mx, E4M3, P, HALF, laid(qm_bf, P, HALF))
+        quantize(dss_mx, E5M2, 0, R, dss_bf[:])
+        quantize(qm_mx, E4M3, HALF, D, laid(qm_bf, HALF, D))
+        for h in range(2):
+            quantize(kt_mx, E4M3, HALF * h, HALF * (h + 1), kt_bf[h][:].rearrange("m j x -> m (j x)"))
         for b in range(1, PACK):
-            key_gradient(b)
+            key_gradient(b, N)
 
         gq_sb = sb("gq_sb", [P, PACK, D], F32, "k_pool0")
         gq_rows = out_0[0].rearrange("(m t) d -> m t d", t=PACK)
         for t in range(PACK):
             gq = bank("turn")
-            matmul(gq, dss_mx, E5, t, kt_mx, E4)
+            matmul(gq[:], dss_mx, E5M2, t, kt_mx, E4M3)
             nc.scalar.copy(
                 gq_sb[:, t, :].rearrange("m (p j) -> m p j", j=PACK),
                 gq[:].rearrange("m (j p) -> m p j", j=PACK),

@@ -23,7 +23,6 @@ HALF = WIDTH // 2
 BAND = 16
 RUN = 4
 BANKS_PER_TAG = 4
-WINDOWS = 3
 DIRECT = 2
 Q_SPLIT = 96
 DO_SPLIT = 88
@@ -91,7 +90,7 @@ def tile_attend_gat_lse_qk_ts_kernel(
         qm_raw = sb("qm_raw", [P, PACK, D], F32)
         ts_pool = sb("ts_pool", [P, T], F32)
         nc.vector.memset(ts_pool[:], 0.0)
-        windows = [sb("window%d" % b, [P, T], F32) for b in range(WINDOWS)]
+        windows = [sb("window%d" % b, [P, T], F32) for b in range(PACK)]
         nc.vector.memset(windows[0][:], 0.0)
         nc.sync.dma_start(ts_pool[0:1, :], ts[0:1, :])
         lse_c = sb("lse_c", [P, PACK], F32)
@@ -244,7 +243,7 @@ def tile_attend_gat_lse_qk_ts_kernel(
         def key_gradient(b, width):
             dk = bank("mm")
             matmul(dk[:], qm_mx, E4M3, b, dsr_mx, E5M2)
-            window = windows[b % WINDOWS]
+            window = windows[b]
             for c0 in range(0, N, width):
                 nc.scalar.copy(dk_sb[:, b, c0 : c0 + width], dk[:, c0 : c0 + width])
             for c0 in range(0, N, width):

@@ -23,9 +23,6 @@ HALF = WIDTH // 2
 BAND = 16
 RUN = 4
 BANKS_PER_TAG = 4
-DIRECT = 2
-Q_SPLIT = 96
-DO_SPLIT = 88
 DS_SPLIT = 352
 
 
@@ -35,6 +32,7 @@ def tile_attend_gat_lse_qk_ts_kernel(
     nc = tc.nc
     with ExitStack() as ctx:
         keep = ctx.enter_context(tc.tile_pool(name="keep", bufs=1))
+        late = ctx.enter_context(tc.tile_pool(name="late", bufs=1))
         psum = ctx.enter_context(tc.psum_pool(name="psum", bufs=BANKS_PER_TAG))
 
         def sb(name, shape, dtype, reuse=None):
@@ -67,13 +65,13 @@ def tile_attend_gat_lse_qk_ts_kernel(
         def gather(out, window, c0=0, c1=N):
             nc.vector.tensor_copy(out, window[:].indirect(offsets[:, c0 // BAND : c1 // BAND]))
 
-        def interleave_views(dst, planes, c0, c1):
+        def interleave_views(dst, c0, c1, planes):
             out = laid(dst, c0, c1).rearrange("p (c i j) -> p c j i", i=RUN, j=PACK)
-            return out, planes[:, :, c0:c1].rearrange("p j (c i) -> p c j i", i=RUN)
+            return out, planes.rearrange("p j (c i) -> p c j i", i=RUN)
 
-        def pair_views(dst, planes, j0, cols):
-            out = dst[:].rearrange("p (c j) -> p c j", j=PACK)[:, cols, j0 : j0 + 2]
-            return out, planes[:, j0 : j0 + 2, cols].rearrange("p j c -> p c j")
+        def pair_views(dst, pair, h, c0=0, c1=N):
+            out = dst[:].rearrange("p (c j) -> p c j", j=PACK)[:, c0:c1, 2 * h : 2 * h + 2]
+            return out, pair[:].rearrange("p (j c) -> p c j", j=2)[:, c0:c1]
 
         def query_views(dst, planes, m0, m1):
             out = dst[:].rearrange("p (t m j) -> p m j t", t=PACK, j=PACK)[:, m0:m1]
@@ -85,60 +83,65 @@ def tile_attend_gat_lse_qk_ts_kernel(
         v_rows = vT.rearrange("(p j) t -> p j t", j=PACK)
         k_pool = [sb("k_pool%d" % j, [P, T], F32) for j in range(PACK)]
         v_pool = [sb("v_pool%d" % j, [P, T], F32) for j in range(PACK)]
-        q_raw = [sb("q_raw%d" % h, [P, PACK, HALF], F32) for h in range(2)]
-        do_raw = sb("do_raw", [P, PACK, R], F32)
-        qm_raw = sb("qm_raw", [P, PACK, D], F32)
+        q_raw = sb("q_raw", [P, PACK, R], F32)
+        do_raw = [sb("do_raw%d" % h, [P, PACK, P], F32) for h in range(PACK)]
+        qm_first = sb("qm_first", [P, PACK, P], F32)
+        qm_rest = late.tile([P, PACK, D - P], F32, name="qm_rest", align_bytes=64, offset=0)
         ts_pool = sb("ts_pool", [P, T], F32)
         nc.vector.memset(ts_pool[:], 0.0)
         windows = [sb("window%d" % b, [P, T], F32) for b in range(PACK)]
         nc.vector.memset(windows[0][:], 0.0)
-        nc.sync.dma_start(ts_pool[0:1, :], ts[0:1, :])
+        ts_raw = sb("ts_raw", [1, T], F32)
+        nc.sync.dma_start(ts_raw[:], ts[0:1, :])
+        nc.scalar.copy(ts_pool[0:1, :], ts_raw[:])
         lse_c = sb("lse_c", [P, PACK], F32)
         delta_c = sb("delta_c", [P, PACK], F32)
         rw_c = sb("rw_c", [P, PACK], F32)
-        token_halves = [slice(0, T // 2), slice(T // 2, T)]
-        for tokens in token_halves:
-            nc.sync.dma_start(k_pool[0][:, tokens], k_rows[:, 0, tokens])
-        for columns, vector in ((lse_c, lse), (delta_c, delta), (rw_c, rw)):
+        nc.sync.dma_start(k_pool[0][:], k_rows[:, 0, :])
+        for columns, vector in ((lse_c, lse), (rw_c, rw)):
             nc.sync.dma_start(columns[:], vector[0].rearrange("(p t) o -> p (t o)", t=PACK))
-        for tokens in token_halves:
-            nc.sync.dma_start(k_pool[1][:, tokens], k_rows[:, 1, tokens])
-        for j in range(2, PACK):
+        for j in range(1, PACK):
             nc.sync.dma_start(k_pool[j][:], k_rows[:, j, :])
-        q_rows = qT[0].rearrange("(p j) r -> p j r", j=PACK)
-        for h in range(2):
-            nc.sync.dma_start(q_raw[h][:], q_rows[:, :, HALF * h : HALF * (h + 1)])
-        for j in range(2):
+        nc.sync.dma_start(q_raw[:], qT[0].rearrange("(p j) r -> p j r", j=PACK))
+        for j in range(PACK):
             nc.sync.dma_start(v_pool[j][:], v_rows[:, j, :])
-        nc.sync.dma_start(do_raw[:], doT[0].rearrange("(p j) r -> p j r", j=PACK))
-        for j in range(2, PACK):
-            nc.sync.dma_start(v_pool[j][:], v_rows[:, j, :])
-        nc.sync.dma_start(qm_raw[:], qm[0].rearrange("(p t) d -> p t d", t=PACK))
+        do_rows = doT[0].rearrange("(p j) r -> p j r", j=PACK)
+        for h in range(PACK):
+            nc.sync.dma_start(do_raw[h][:], do_rows[:, :, P * h : P * (h + 1)])
+        nc.sync.dma_start(delta_c[:], delta[0].rearrange("(p t) o -> p (t o)", t=PACK))
+        qm_rows = qm[0].rearrange("(p t) d -> p t d", t=PACK)
+        nc.sync.dma_start(qm_first[:], qm_rows[:, :, 0:P])
+        nc.sync.dma_start(qm_rest[:], qm_rows[:, :, P:D])
 
         ident = sb("ident", [P, P], F32)
         make_identity(nc, ident[:])
         for window in windows[1:]:
             nc.gpsimd.memset(window[:], 0.0)
 
-        k_g = sb("k_g", [P, PACK, N], F32)
-        kt_bf = [sb("kt_bf0", [P, 2, WIDTH], BF16)]
-        kt_mx = mx_tiles("kt")
+        k_g = [sb("k_g%d" % h, [P, 2 * N], BF16) for h in range(2)]
+        kt_bf = [sb("kt_bf0", [P, HALF * PACK], BF16)]
 
-        def turn_keys(j):
+        def turn_pairs(turned, column, plane):
+            words = plane.bitcast(F32)
+            for u in range(2):
+                nc.tensor.transpose(turned[:, column + P * u : column + P * (u + 1)], words[:, u::2], ident[:])
+
+        def turn_keys(h):
             turned = bank("turn")
-            for t in range(PACK):
-                nc.tensor.transpose(turned[:, P * t : P * (t + 1)], k_g[:, j, t::PACK], ident[:])
+            for e in range(2):
+                turn_pairs(turned, HALF * e, k_g[h][:, N * e : N * (e + 1)])
             nc.scalar.copy(
-                kt_bf[j // 2][:, j % 2, :].rearrange("m (p t) -> m p t", t=PACK),
-                turned[:].rearrange("m (t p) -> m p t", t=PACK),
+                kt_bf[h][:].bitcast(F32).rearrange("m (e p u) -> m e p u", e=2, u=2),
+                turned[:].rearrange("m (e u p) -> m e p u", e=2, u=2),
             )
 
+        def gather_plane(pairs, pool, j):
+            gather(pairs[j // 2][:, N * (j % 2) : N * (j % 2 + 1)], pool[j])
+
         for j in range(2):
-            gather(k_g[:, j, :], k_pool[j])
-            turn_keys(j)
-        all_slots = slice(0, N)
+            gather_plane(k_g, k_pool, j)
         k_bf = sb("k_bf", [P, N * PACK], BF16)
-        nc.vector.tensor_copy(*pair_views(k_bf, k_g, 0, all_slots))
+        nc.scalar.copy(*pair_views(k_bf, k_g[0], 0))
 
         ts_g = sb("ts_g", [P, N], F32)
         gather(ts_g[:], ts_pool)
@@ -152,128 +155,156 @@ def tile_attend_gat_lse_qk_ts_kernel(
             nc.tensor.transpose(turned[:, P * s : P * (s + 1)], ts_col[:, s : s + 1].to_broadcast([P, P]), ident[:])
         ts_row = sb("ts_row", [P, N], F32)
         nc.scalar.copy(ts_row[:], turned[:])
+        ts_rw = sb("ts_rw", [P, N], F32)
+        nc.scalar.activation(ts_rw[:], turned[:], ACT.Copy, scale=rw_c[:, PACK - 1 : PACK])
         neg_lse = sb("neg_lse", [P, PACK], F32)
         nc.vector.tensor_scalar(neg_lse[:], lse_c[:], -1.0, None, ALU.mult)
 
+        turn_keys(0)
         for j in range(2, PACK):
-            gather(k_g[:, j, :], k_pool[j])
+            gather_plane(k_g, k_pool, j)
         k_mx = mx_tiles("k")
-        nc.vector.tensor_copy(*pair_views(k_bf, k_g, 2, all_slots))
+        nc.vector.tensor_copy(*pair_views(k_bf, k_g[1], 1))
         quantize(k_mx, E4M3, 0, N, k_bf[:])
 
-        q_bf = sb("q_bf", [P, R * PACK], BF16, "k_pool3")
+        q_bf = sb("q_bf", [P, R * PACK], BF16)
         q_mx = mx_tiles("q")
-        q_cut = PACK * Q_SPLIT - HALF
-        nc.scalar.copy(*query_views(q_bf, q_raw[0][:], 0, P // 2))
-        nc.scalar.copy(*query_views(q_bf, q_raw[1][:, :, 0:q_cut], P // 2, Q_SPLIT))
-        nc.vector.tensor_copy(*query_views(q_bf, q_raw[1][:, :, q_cut:HALF], Q_SPLIT, P))
+        nc.scalar.copy(*interleave_views(q_bf, 0, HALF, q_raw[:, :, 0:HALF]))
+        nc.vector.tensor_copy(*interleave_views(q_bf, HALF, R, q_raw[:, :, HALF:R]))
         quantize(q_mx, E4M3, 0, R, q_bf[:])
-        kt_bf.append(sb("kt_bf1", [P, 2, WIDTH], BF16, "q_raw1"))
-        for j in range(2, PACK):
-            turn_keys(j)
+        kt_bf.append(sb("kt_bf1", [P, HALF * PACK], BF16, "q_raw"))
+        turn_keys(1)
 
-        a_direct = sb("a_direct", [P, DIRECT, N], F32)
-        v_g = sb("v_g", [P, PACK, N], F32, "k_pool3")
-        a_slots = sb("a_slots", [P, PACK, HALF], F32)
+        v_g = sb("v_g", [P, 2 * N], BF16)
+        v_bf = sb("v_bf", [P, N * PACK], BF16)
+        v_places = v_bf[:].rearrange("p (c j) -> p c j", j=PACK)
+        a_slots = sb("a_slots", [P, PACK, R], F32)
         a_banks = [bank("turn") for t in range(PACK)]
-        for t in range(DIRECT):
-            matmul(a_banks[t][:], q_mx, E4M3, t, k_mx, E4M3)
-        slot_banks = [bank("mm") for s in range(PACK)]
         for s in range(PACK):
-            matmul(slot_banks[s][:, 0:HALF], k_mx, E4M3, s, q_mx, E4M3, P * DIRECT)
-        for t in range(DIRECT):
-            nc.vector.tensor_tensor(a_direct[:, t, :], a_banks[t][:], ts_row[:], ALU.mult)
+            scores = bank("mm")
+            matmul(scores[:], k_mx, E4M3, s, q_mx, E4M3)
+            nc.scalar.activation(
+                a_slots[:, s, :].rearrange("p (t m) -> p t m", t=PACK),
+                scores[:].rearrange("p (m t) -> p t m", t=PACK),
+                ACT.Copy,
+                scale=ts_col[:, s : s + 1],
+            )
         for s in range(PACK):
-            nc.scalar.activation(a_slots[:, s, :], slot_banks[s][:, 0:HALF], ACT.Copy, scale=ts_col[:, s : s + 1])
-        for t in range(DIRECT, PACK):
-            queries = slice(P * (t - DIRECT), P * (t - DIRECT + 1))
-            for s in range(PACK):
-                nc.tensor.transpose(a_banks[t][:, P * s : P * (s + 1)], a_slots[:, s, queries], ident[:])
+            for t in range(PACK):
+                nc.tensor.transpose(
+                    a_banks[t][:, P * s : P * (s + 1)], a_slots[:, s, P * t : P * (t + 1)], ident[:]
+                )
         p_sb = [sb("p_sb%d" % t, [P, N], F32) for t in range(PACK)]
         for t in range(PACK):
-            scaled = a_direct[:, t, :] if t < DIRECT else a_banks[t][:]
-            nc.scalar.activation(p_sb[t][:], scaled, ACT.Exp, bias=neg_lse[:, t : t + 1])
+            nc.scalar.activation(p_sb[t][:], a_banks[t][:], ACT.Exp, bias=neg_lse[:, t : t + 1])
 
-        for j in range(2):
-            gather(v_g[:, j, :], v_pool[j])
-        w_sb = [sb("w_sb%d" % t, [P, N], F32) for t in range(PACK)]
-        for t in range(PACK):
-            nc.vector.scalar_tensor_tensor(
-                w_sb[t][:], p_sb[t][:], rw_c[:, t : t + 1], ts_row[:], ALU.mult, ALU.mult
-            )
-        do_bf = sb("do_bf", [P, R * PACK], BF16, "neg_lse")
-        nc.scalar.copy(*query_views(do_bf, do_raw[:, :, 0 : PACK * DO_SPLIT], 0, DO_SPLIT))
-        v_bf = sb("v_bf", [P, N * PACK], BF16, "a_slots")
+        def weigh(w, t):
+            nc.vector.scalar_tensor_tensor(w, p_sb[t][:], rw_c[:, t : t + 1], ts_row[:], ALU.mult, ALU.mult)
+
+        gather(v_places[:, :, 0], v_pool[0])
+        kt_mx = mx_tiles("kt", "v_pool0")
+        for h in range(2):
+            quantize(kt_mx, E4M3, HALF * h, HALF * (h + 1), kt_bf[h][:])
+        gather(v_places[:, :, 1], v_pool[1])
+        gather(v_g[:, 0:N], v_pool[2])
+        w_pair = sb("w_pair", [P, 2 * N], F32, "v_pool2")
+        w_sb = [w_pair[:, 0:N], w_pair[:, N : 2 * N]]
+        for t in range(2):
+            weigh(w_sb[t], t)
+        w_last = sb("w_last", [P, N], F32, "p_sb1")
+        nc.gpsimd.tensor_tensor(w_last[:], p_sb[PACK - 1][:], ts_rw[:], ALU.mult)
         v_mx = mx_tiles("v")
-        nc.scalar.copy(*pair_views(v_bf, v_g, 0, all_slots))
-        gather(v_g[:, 2, :], v_pool[2])
-        nc.vector.tensor_copy(*query_views(do_bf, do_raw[:, :, PACK * DO_SPLIT : R], DO_SPLIT, P))
         for c0 in (0, HALF):
-            slots = slice(c0, c0 + HALF)
-            gather(v_g[:, 3, slots], v_pool[3], c0, c0 + HALF)
-            nc.scalar.copy(*pair_views(v_bf, v_g, 2, slots))
-        do_mx = mx_tiles("do", "v_pool3")
-        quantize(do_mx, E5M2, 0, R, do_bf[:])
+            gather(v_g[:, N + c0 : N + c0 + HALF], v_pool[3], c0, c0 + HALF)
+        for c0 in (0, HALF):
+            nc.vector.tensor_copy(*pair_views(v_bf, v_g, 1, c0, c0 + HALF))
         for c0 in (0, HALF):
             quantize(v_mx, E4M3, c0, c0 + HALF, laid(v_bf, c0, c0 + HALF))
+        do_bf = sb("do_bf", [P, R * PACK], BF16)
+        grad_codes = sb("grad_codes", [P, 2 * WIDTH], U32)
+        grad_scales = sb("grad_scales", [P, 2 * WIDTH], U8)
+        do_mx = grad_codes[:, 0:WIDTH], grad_scales[:, 0:WIDTH]
+        dsr_mx = grad_codes[:, WIDTH : 2 * WIDTH], grad_scales[:, WIDTH : 2 * WIDTH]
+        early_mx = grad_codes[:, HALF : HALF + WIDTH], grad_scales[:, HALF : HALF + WIDTH]
+        for h in range(PACK):
+            nc.scalar.copy(*query_views(do_bf, do_raw[h][:], P // PACK * h, P // PACK * (h + 1)))
+        w_third = sb("w_third", [P, N], F32, "v_pool3")
+        weigh(w_third[:], 2)
+        w_sb.extend([w_third[:], w_last[:]])
+        for t in range(PACK):
+            quantize(do_mx, E5M2, P * t, P * (t + 1), laid(do_bf, P * t, P * (t + 1)))
 
-        qm_bf = sb("qm_bf", [P, D * PACK], BF16, "k_pool3")
-        qm_mx = mx_tiles("qm", "a_slots")
-        nc.scalar.copy(*interleave_views(qm_bf, qm_raw, 0, P))
+        qm_bf = sb("qm_bf", [P, D * PACK], BF16)
+        qm_mx = mx_tiles("qm")
+        nc.scalar.copy(*interleave_views(qm_bf, 0, P, qm_first[:]))
         quantize(qm_mx, E4M3, 0, P, laid(qm_bf, 0, P))
 
-        ds_bf = sb("ds_bf", [P, PACK, N], BF16)
+        ds_bf = sb("ds_bf", [P, PACK * N], BF16, "qm_first")
+        dp = [bank("mm") for t in range(PACK)]
         for t in range(PACK):
-            dp = bank("mm")
-            matmul(dp[:], do_mx, E5M2, t, v_mx, E4M3)
+            matmul(dp[t][:], do_mx, E5M2, t, v_mx, E4M3)
+
+        def gradient(t, c0, c1):
             nc.vector.scalar_tensor_tensor(
-                ds_bf[:, t, :], dp[:], delta_c[:, t : t + 1], w_sb[t][:], ALU.subtract, ALU.mult
+                ds_bf[:, N * t + c0 : N * t + c1],
+                dp[t][:, c0:c1],
+                delta_c[:, t : t + 1],
+                w_sb[t][:, c0:c1],
+                ALU.subtract,
+                ALU.mult,
             )
 
-        dsr_bf = sb("dsr_bf", [P, N * PACK], BF16)
-        dsr_mx = mx_tiles("dsr")
-        nc.scalar.copy(*interleave_views(dsr_bf, ds_bf, DS_SPLIT, N))
-        nc.vector.tensor_copy(*interleave_views(dsr_bf, ds_bf, 0, HALF))
-        nc.vector.tensor_copy(*interleave_views(dsr_bf, ds_bf, HALF, DS_SPLIT))
+        for t in range(PACK - 1):
+            gradient(t, 0, N)
         for c0 in (0, HALF):
-            quantize(dsr_mx, E5M2, c0, c0 + HALF, laid(dsr_bf, c0, c0 + HALF))
+            gradient(PACK - 1, c0, c0 + HALF)
+
+        for b in range(1, PACK):
+            nc.scalar.copy(*interleave_views(qm_bf, P * b, P * (b + 1), qm_rest[:, :, P * (b - 1) : P * b]))
+
+        dsr_bf = late.tile([P, N * PACK], BF16, name="dsr_bf", align_bytes=64, offset=0)
+        ds_planes = ds_bf[:].rearrange("p (t i) -> p t i", t=PACK)
+        nc.vector.tensor_copy(*interleave_views(dsr_bf, 0, HALF, ds_planes[:, :, 0:HALF]))
+        nc.vector.tensor_copy(*interleave_views(dsr_bf, HALF, DS_SPLIT, ds_planes[:, :, HALF:DS_SPLIT]))
+        quantize(dsr_mx, E5M2, 0, HALF, laid(dsr_bf, 0, HALF))
 
         dk_sb = sb("dk_sb", [P, PACK, N], F32, "k_pool1")
 
-        def key_gradient(b, width):
+        def scatter(b, c0, c1, dk):
+            nc.scalar.copy(dk_sb[:, b, c0:c1], dk)
+            nc.vector.tensor_copy(
+                windows[b][:].indirect(offsets[:, c0 // BAND : c1 // BAND]), dk_sb[:, b, c0:c1]
+            )
+
+        early = bank("mm")
+        matmul(early[:], qm_mx, E4M3, 0, early_mx, E5M2)
+        nc.scalar.copy(*interleave_views(dsr_bf, DS_SPLIT, N, ds_planes[:, :, DS_SPLIT:N]))
+        quantize(dsr_mx, E5M2, HALF, N, laid(dsr_bf, HALF, N))
+        scatter(0, 0, HALF, early[:, HALF:WIDTH])
+
+        def key_gradient(b, c0):
             dk = bank("mm")
             matmul(dk[:], qm_mx, E4M3, b, dsr_mx, E5M2)
-            window = windows[b]
-            for c0 in range(0, N, width):
-                nc.scalar.copy(dk_sb[:, b, c0 : c0 + width], dk[:, c0 : c0 + width])
-            for c0 in range(0, N, width):
-                nc.vector.tensor_copy(
-                    window[:].indirect(offsets[:, c0 // BAND : (c0 + width) // BAND]), dk_sb[:, b, c0 : c0 + width]
-                )
-            nc.sync.dma_start(out_1[P * b : P * (b + 1), :], window[:])
+            scatter(b, c0, N, dk[:, c0:N])
+            nc.sync.dma_start(out_1[P * b : P * (b + 1), :], windows[b][:])
 
-        key_gradient(0, HALF)
-
-        dss_bf = sb("dss_bf", [P, R * PACK], BF16)
+        dss_bf = late.tile([P, R * PACK], BF16, name="dss_bf", align_bytes=64, offset=2 * N * PACK)
         dss_mx = mx_tiles("dss")
         for t in range(PACK):
-            words = ds_bf[:, t, :].bitcast(F32)
             turned = bank("turn")
-            for u in range(2):
-                nc.tensor.transpose(turned[:, P * u : P * (u + 1)], words[:, u::2], ident[:])
+            turn_pairs(turned, 0, ds_bf[:, N * t : N * (t + 1)])
             nc.scalar.copy(
                 laid(dss_bf, P * t, P * (t + 1)).bitcast(F32).rearrange("p (m u) -> p m u", u=2),
                 turned[:, 0 : 2 * P].rearrange("p (u m) -> p m u", u=2),
             )
-        for b in range(1, PACK):
-            nc.scalar.copy(*interleave_views(qm_bf, qm_raw, P * b, P * (b + 1)))
         quantize(qm_mx, E4M3, P, HALF, laid(qm_bf, P, HALF))
-        quantize(dss_mx, E5M2, 0, R, dss_bf[:])
         quantize(qm_mx, E4M3, HALF, D, laid(qm_bf, HALF, D))
-        for h in range(2):
-            quantize(kt_mx, E4M3, HALF * h, HALF * (h + 1), kt_bf[h][:].rearrange("m j x -> m (j x)"))
-        for b in range(1, PACK):
-            key_gradient(b, N)
+        for c0 in (0, HALF):
+            quantize(dss_mx, E5M2, c0, c0 + HALF, laid(dss_bf, c0, c0 + HALF))
+        key_gradient(1, 0)
+        key_gradient(0, HALF)
+        for b in range(2, PACK):
+            key_gradient(b, 0)
 
         gq_sb = sb("gq_sb", [P, PACK, D], F32, "k_pool0")
         gq_rows = out_0[0].rearrange("(m t) d -> m t d", t=PACK)

@@ -23,7 +23,6 @@ HALF = WIDTH // 2
 BAND = 16
 RUN = 4
 BANKS_PER_TAG = 4
-DS_SPLIT = 352
 
 
 def tile_attend_gat_lse_qk_ts_kernel(
@@ -32,7 +31,6 @@ def tile_attend_gat_lse_qk_ts_kernel(
     nc = tc.nc
     with ExitStack() as ctx:
         keep = ctx.enter_context(tc.tile_pool(name="keep", bufs=1))
-        late = ctx.enter_context(tc.tile_pool(name="late", bufs=1))
         psum = ctx.enter_context(tc.psum_pool(name="psum", bufs=BANKS_PER_TAG))
 
         def sb(name, shape, dtype, reuse=None):
@@ -50,14 +48,14 @@ def tile_attend_gat_lse_qk_ts_kernel(
         def laid(tile, c0, c1):
             return tile[:, PACK * c0 : PACK * c1]
 
-        def matmul(out, stationary, stationary_fmt, block, moving, moving_fmt, c0=0):
+        def matmul(out, stationary, stationary_fmt, block, moving, moving_fmt, c0=0, c1=WIDTH):
             cols = slice(P * block, P * (block + 1))
             nc.tensor.matmul_mx(
                 out=out,
                 lhsT=stationary[0][:, cols].bitcast(stationary_fmt),
                 lhsT_scale=stationary[1][:, cols],
-                rhs=moving[0][:, c0:WIDTH].bitcast(moving_fmt),
-                rhs_scale=moving[1][:, c0:WIDTH],
+                rhs=moving[0][:, c0:c1].bitcast(moving_fmt),
+                rhs_scale=moving[1][:, c0:c1],
                 start=True,
                 stop=True,
             )
@@ -85,8 +83,7 @@ def tile_attend_gat_lse_qk_ts_kernel(
         v_pool = [sb("v_pool%d" % j, [P, T], F32) for j in range(PACK)]
         q_raw = sb("q_raw", [P, PACK, R], F32)
         do_raw = [sb("do_raw%d" % h, [P, PACK, P], F32) for h in range(PACK)]
-        qm_first = sb("qm_first", [P, PACK, P], F32)
-        qm_rest = late.tile([P, PACK, D - P], F32, name="qm_rest", align_bytes=64, offset=0)
+        qm_raw = [sb("qm_raw%d" % b, [P, PACK, P], F32) for b in range(PACK)]
         ts_pool = sb("ts_pool", [P, T], F32)
         nc.vector.memset(ts_pool[:], 0.0)
         windows = [sb("window%d" % b, [P, T], F32) for b in range(PACK)]
@@ -110,8 +107,8 @@ def tile_attend_gat_lse_qk_ts_kernel(
             nc.sync.dma_start(do_raw[h][:], do_rows[:, :, P * h : P * (h + 1)])
         nc.sync.dma_start(delta_c[:], delta[0].rearrange("(p t) o -> p (t o)", t=PACK))
         qm_rows = qm[0].rearrange("(p t) d -> p t d", t=PACK)
-        nc.sync.dma_start(qm_first[:], qm_rows[:, :, 0:P])
-        nc.sync.dma_start(qm_rest[:], qm_rows[:, :, P:D])
+        for b in range(PACK):
+            nc.sync.dma_start(qm_raw[b][:], qm_rows[:, :, P * b : P * (b + 1)])
 
         ident = sb("ident", [P, P], F32)
         make_identity(nc, ident[:])
@@ -221,11 +218,7 @@ def tile_attend_gat_lse_qk_ts_kernel(
         for c0 in (0, HALF):
             quantize(v_mx, E4M3, c0, c0 + HALF, laid(v_bf, c0, c0 + HALF))
         do_bf = sb("do_bf", [P, R * PACK], BF16)
-        grad_codes = sb("grad_codes", [P, 2 * WIDTH], U32)
-        grad_scales = sb("grad_scales", [P, 2 * WIDTH], U8)
-        do_mx = grad_codes[:, 0:WIDTH], grad_scales[:, 0:WIDTH]
-        dsr_mx = grad_codes[:, WIDTH : 2 * WIDTH], grad_scales[:, WIDTH : 2 * WIDTH]
-        early_mx = grad_codes[:, HALF : HALF + WIDTH], grad_scales[:, HALF : HALF + WIDTH]
+        do_mx = mx_tiles("do")
         for h in range(PACK):
             nc.scalar.copy(*query_views(do_bf, do_raw[h][:], P // PACK * h, P // PACK * (h + 1)))
         w_third = sb("w_third", [P, N], F32, "v_pool3")
@@ -236,83 +229,112 @@ def tile_attend_gat_lse_qk_ts_kernel(
 
         qm_bf = sb("qm_bf", [P, D * PACK], BF16)
         qm_mx = mx_tiles("qm")
-        nc.scalar.copy(*interleave_views(qm_bf, 0, P, qm_first[:]))
-        quantize(qm_mx, E4M3, 0, P, laid(qm_bf, 0, P))
 
-        ds_bf = sb("ds_bf", [P, PACK * N], BF16, "qm_first")
+        def lay_qm(b):
+            nc.scalar.copy(*interleave_views(qm_bf, P * b, P * (b + 1), qm_raw[b][:]))
+
+        def quantize_block(mx, fmt, tile, b0, b1):
+            quantize(mx, fmt, P * b0, P * b1, laid(tile, P * b0, P * b1))
+
+        ds_bf = sb("ds_bf", [P, PACK * N], BF16)
+        ds_planes = ds_bf[:].rearrange("p (t i) -> p t i", t=PACK)
         dp = [bank("mm") for t in range(PACK)]
-        for t in range(PACK):
-            matmul(dp[t][:], do_mx, E5M2, t, v_mx, E4M3)
 
-        def gradient(t, c0, c1):
+        def gradient(t, c0):
+            matmul(dp[t][:, c0 : c0 + HALF], do_mx, E5M2, t, v_mx, E4M3, c0, c0 + HALF)
             nc.vector.scalar_tensor_tensor(
-                ds_bf[:, N * t + c0 : N * t + c1],
-                dp[t][:, c0:c1],
+                ds_bf[:, N * t + c0 : N * t + c0 + HALF],
+                dp[t][:, c0 : c0 + HALF],
                 delta_c[:, t : t + 1],
-                w_sb[t][:, c0:c1],
+                w_sb[t][:, c0 : c0 + HALF],
                 ALU.subtract,
                 ALU.mult,
             )
 
-        for t in range(PACK - 1):
-            gradient(t, 0, N)
-        for c0 in (0, HALF):
-            gradient(PACK - 1, c0, c0 + HALF)
-
-        for b in range(1, PACK):
-            nc.scalar.copy(*interleave_views(qm_bf, P * b, P * (b + 1), qm_rest[:, :, P * (b - 1) : P * b]))
-
-        dsr_bf = late.tile([P, N * PACK], BF16, name="dsr_bf", align_bytes=64, offset=0)
-        ds_planes = ds_bf[:].rearrange("p (t i) -> p t i", t=PACK)
-        nc.vector.tensor_copy(*interleave_views(dsr_bf, 0, HALF, ds_planes[:, :, 0:HALF]))
-        nc.vector.tensor_copy(*interleave_views(dsr_bf, HALF, DS_SPLIT, ds_planes[:, :, HALF:DS_SPLIT]))
-        quantize(dsr_mx, E5M2, 0, HALF, laid(dsr_bf, 0, HALF))
-
-        dk_sb = sb("dk_sb", [P, PACK, N], F32, "k_pool1")
-
-        def scatter(b, c0, c1, dk):
-            nc.scalar.copy(dk_sb[:, b, c0:c1], dk)
-            nc.vector.tensor_copy(
-                windows[b][:].indirect(offsets[:, c0 // BAND : c1 // BAND]), dk_sb[:, b, c0:c1]
-            )
-
-        early = bank("mm")
-        matmul(early[:], qm_mx, E4M3, 0, early_mx, E5M2)
-        nc.scalar.copy(*interleave_views(dsr_bf, DS_SPLIT, N, ds_planes[:, :, DS_SPLIT:N]))
-        quantize(dsr_mx, E5M2, HALF, N, laid(dsr_bf, HALF, N))
-        scatter(0, 0, HALF, early[:, HALF:WIDTH])
-
-        def key_gradient(b, c0):
-            dk = bank("mm")
-            matmul(dk[:], qm_mx, E4M3, b, dsr_mx, E5M2)
-            scatter(b, c0, N, dk[:, c0:N])
-            nc.sync.dma_start(out_1[P * b : P * (b + 1), :], windows[b][:])
-
-        dss_bf = late.tile([P, R * PACK], BF16, name="dss_bf", align_bytes=64, offset=2 * N * PACK)
+        dsr_bf = sb("dsr_bf", [P, N * PACK], BF16)
+        dsr_mx = mx_tiles("dsr")
+        dss_bf = sb("dss_bf", [P, R * PACK], BF16)
         dss_mx = mx_tiles("dss")
-        for t in range(PACK):
+
+        def turn_gradient(t):
             turned = bank("turn")
             turn_pairs(turned, 0, ds_bf[:, N * t : N * (t + 1)])
             nc.scalar.copy(
                 laid(dss_bf, P * t, P * (t + 1)).bitcast(F32).rearrange("p (m u) -> p m u", u=2),
                 turned[:, 0 : 2 * P].rearrange("p (u m) -> p m u", u=2),
             )
-        quantize(qm_mx, E4M3, P, HALF, laid(qm_bf, P, HALF))
-        quantize(qm_mx, E4M3, HALF, D, laid(qm_bf, HALF, D))
-        for c0 in (0, HALF):
-            quantize(dss_mx, E5M2, c0, c0 + HALF, laid(dss_bf, c0, c0 + HALF))
-        key_gradient(1, 0)
-        key_gradient(0, HALF)
-        for b in range(2, PACK):
-            key_gradient(b, 0)
 
-        gq_sb = sb("gq_sb", [P, PACK, D], F32, "k_pool0")
+        dk_sb = [sb("dk_sb%d" % b, [P, N], F32) for b in range(PACK)]
+        gq_sb = [sb("gq_sb%d" % t, [P, D], F32) for t in range(2)]
         gq_rows = out_0[0].rearrange("(m t) d -> m t d", t=PACK)
-        for t in range(PACK):
+
+        def key_gradient(copy, b, c0, c1):
+            dk = bank("mm")
+            matmul(dk[:, c0:c1], qm_mx, E4M3, b, dsr_mx, E5M2, c0, c1)
+            copy(dk_sb[b][:, c0:c1], dk[:, c0:c1])
+
+        def places(b, c0, c1):
+            return windows[b][:].indirect(offsets[:, c0 // BAND : c1 // BAND])
+
+        def scatter_on_scalar(b, c0):
+            nc.scalar.activation(places(b, c0, c0 + HALF), dk_sb[b][:, c0 : c0 + HALF], ACT.Copy)
+
+        def scatter_on_vector(b):
+            nc.vector.tensor_copy(places(b, 0, N), dk_sb[b][:])
+
+        def store_window(b):
+            nc.sync.dma_start(out_1[P * b : P * (b + 1), :], windows[b][:])
+
+        def query_gradient(copy, t):
             gq = bank("turn")
             matmul(gq[:], dss_mx, E5M2, t, kt_mx, E4M3)
-            nc.scalar.copy(
-                gq_sb[:, t, :].rearrange("m (p j) -> m p j", j=PACK),
+            copy(
+                gq_sb[t][:].rearrange("m (p j) -> m p j", j=PACK),
                 gq[:].rearrange("m (j p) -> m p j", j=PACK),
             )
-            nc.scalar.dma_start(gq_rows[:, t, :], gq_sb[:, t, :])
+            nc.scalar.dma_start(gq_rows[:, t, :], gq_sb[t][:])
+
+        for b in range(PACK - 1):
+            lay_qm(b)
+        for t in range(PACK):
+            gradient(t, 0)
+        gradient(0, HALF)
+        nc.vector.tensor_copy(*interleave_views(dsr_bf, 0, P, ds_planes[:, :, 0:P]))
+        nc.scalar.copy(*interleave_views(dsr_bf, P, HALF, ds_planes[:, :, P:HALF]))
+        lay_qm(PACK - 1)
+        gradient(1, HALF)
+        quantize_block(qm_mx, E4M3, qm_bf, 0, 1)
+        quantize_block(dsr_mx, E5M2, dsr_bf, 0, 2)
+        gradient(2, HALF)
+        gradient(3, HALF)
+        turn_gradient(0)
+        turn_gradient(1)
+        key_gradient(nc.scalar.copy, 0, 0, HALF)
+        turn_gradient(2)
+        turn_gradient(3)
+        scatter_on_scalar(0, 0)
+        quantize_block(dss_mx, E5M2, dss_bf, 0, 2)
+        nc.vector.tensor_copy(*interleave_views(dsr_bf, HALF, N, ds_planes[:, :, HALF:N]))
+        quantize_block(qm_mx, E4M3, qm_bf, 1, 2)
+        quantize_block(dsr_mx, E5M2, dsr_bf, 2, 4)
+        query_gradient(nc.vector.tensor_copy, 0)
+        key_gradient(nc.vector.tensor_copy, 0, HALF, N)
+        scatter_on_scalar(0, HALF)
+        store_window(0)
+        quantize_block(dss_mx, E5M2, dss_bf, 2, 4)
+        query_gradient(nc.vector.tensor_copy, 1)
+        quantize_block(qm_mx, E4M3, qm_bf, 2, 4)
+        key_gradient(nc.vector.tensor_copy, 1, 0, N)
+        scatter_on_vector(1)
+        store_window(1)
+        key_gradient(nc.scalar.copy, 2, 0, N)
+        for c0 in (0, HALF):
+            scatter_on_scalar(2, c0)
+        store_window(2)
+        gq_late = sb("gq_late", [P, 2 * D], F32, "dk_sb2")
+        gq_sb.extend([gq_late[:, 0:D], gq_late[:, D : 2 * D]])
+        for t in range(2, PACK):
+            query_gradient(nc.scalar.copy, t)
+        key_gradient(nc.vector.tensor_copy, 3, 0, N)
+        scatter_on_vector(3)
+        store_window(3)

@@ -22,6 +22,7 @@ WIDTH = 512
 HALF = WIDTH // 2
 BAND = 16
 RUN = 4
+Q_SPLIT = 48
 BANKS_PER_TAG = 4
 
 
@@ -63,6 +64,9 @@ def tile_attend_gat_lse_qk_ts_kernel(
         def gather(out, window, c0=0, c1=N):
             nc.vector.tensor_copy(out, window[:].indirect(offsets[:, c0 // BAND : c1 // BAND]))
 
+        def gather_on_scalar(out, window, c0=0, c1=N):
+            nc.scalar.activation(out, window[:].indirect(offsets[:, c0 // BAND : c1 // BAND]), ACT.Copy)
+
         def interleave_views(dst, c0, c1, planes):
             out = laid(dst, c0, c1).rearrange("p (c i j) -> p c j i", i=RUN, j=PACK)
             return out, planes.rearrange("p j (c i) -> p c j i", i=RUN)
@@ -87,10 +91,9 @@ def tile_attend_gat_lse_qk_ts_kernel(
         ts_pool = sb("ts_pool", [P, T], F32)
         nc.vector.memset(ts_pool[:], 0.0)
         windows = [sb("window%d" % b, [P, T], F32) for b in range(PACK)]
-        nc.vector.memset(windows[0][:], 0.0)
         ts_raw = sb("ts_raw", [1, T], F32)
         nc.sync.dma_start(ts_raw[:], ts[0:1, :])
-        nc.scalar.copy(ts_pool[0:1, :], ts_raw[:])
+        nc.vector.tensor_copy(ts_pool[0:1, :], ts_raw[:])
         lse_c = sb("lse_c", [P, PACK], F32)
         delta_c = sb("delta_c", [P, PACK], F32)
         rw_c = sb("rw_c", [P, PACK], F32)
@@ -112,7 +115,7 @@ def tile_attend_gat_lse_qk_ts_kernel(
 
         ident = sb("ident", [P, P], F32)
         make_identity(nc, ident[:])
-        for window in windows[1:]:
+        for window in windows:
             nc.gpsimd.memset(window[:], 0.0)
 
         k_g = [sb("k_g%d" % h, [P, 2 * N], BF16) for h in range(2)]
@@ -135,10 +138,8 @@ def tile_attend_gat_lse_qk_ts_kernel(
         def gather_plane(pairs, pool, j):
             gather(pairs[j // 2][:, N * (j % 2) : N * (j % 2 + 1)], pool[j])
 
-        for j in range(2):
-            gather_plane(k_g, k_pool, j)
-        k_bf = sb("k_bf", [P, N * PACK], BF16)
-        nc.scalar.copy(*pair_views(k_bf, k_g[0], 0))
+        neg_lse = sb("neg_lse", [P, PACK], F32)
+        nc.scalar.activation(neg_lse[:], lse_c[:], ACT.Copy, scale=-1.0)
 
         ts_g = sb("ts_g", [P, N], F32)
         gather(ts_g[:], ts_pool)
@@ -152,67 +153,62 @@ def tile_attend_gat_lse_qk_ts_kernel(
             nc.tensor.transpose(turned[:, P * s : P * (s + 1)], ts_col[:, s : s + 1].to_broadcast([P, P]), ident[:])
         ts_row = sb("ts_row", [P, N], F32)
         nc.scalar.copy(ts_row[:], turned[:])
-        ts_rw = sb("ts_rw", [P, N], F32)
-        nc.scalar.activation(ts_rw[:], turned[:], ACT.Copy, scale=rw_c[:, PACK - 1 : PACK])
-        neg_lse = sb("neg_lse", [P, PACK], F32)
-        nc.vector.tensor_scalar(neg_lse[:], lse_c[:], -1.0, None, ALU.mult)
+        ts_rw = sb("ts_rw", [P, 2 * N], F32)
+        for t in range(2, PACK):
+            nc.scalar.activation(ts_rw[:, N * (t - 2) : N * (t - 1)], turned[:], ACT.Copy, scale=rw_c[:, t : t + 1])
 
-        turn_keys(0)
-        for j in range(2, PACK):
+        for j in range(2):
             gather_plane(k_g, k_pool, j)
+        k_bf = sb("k_bf", [P, N * PACK], BF16)
+        nc.vector.tensor_copy(*pair_views(k_bf, k_g[0], 0))
+        turn_keys(0)
+        kt_mx = mx_tiles("kt")
+        gather_plane(k_g, k_pool, 2)
+        quantize(kt_mx, E4M3, 0, HALF, kt_bf[0][:])
+        gather(k_g[1][:, N : N + HALF], k_pool[3], 0, HALF)
+        gather_on_scalar(k_g[1][:, N + HALF : 2 * N], k_pool[3], HALF, N)
         k_mx = mx_tiles("k")
         nc.vector.tensor_copy(*pair_views(k_bf, k_g[1], 1))
         quantize(k_mx, E4M3, 0, N, k_bf[:])
+        kt_bf.append(sb("kt_bf1", [P, HALF * PACK], BF16))
+        turn_keys(1)
 
         q_bf = sb("q_bf", [P, R * PACK], BF16)
         q_mx = mx_tiles("q")
-        nc.scalar.copy(*interleave_views(q_bf, 0, HALF, q_raw[:, :, 0:HALF]))
-        nc.vector.tensor_copy(*interleave_views(q_bf, HALF, R, q_raw[:, :, HALF:R]))
-        quantize(q_mx, E4M3, 0, R, q_bf[:])
-        kt_bf.append(sb("kt_bf1", [P, HALF * PACK], BF16, "q_raw"))
-        turn_keys(1)
+        nc.scalar.copy(*query_views(q_bf, q_raw[:, :, 0 : PACK * Q_SPLIT], 0, Q_SPLIT))
+        nc.vector.tensor_copy(*query_views(q_bf, q_raw[:, :, PACK * Q_SPLIT : R], Q_SPLIT, P))
+        for t in range(PACK):
+            quantize(q_mx, E4M3, P * t, P * (t + 1), laid(q_bf, P * t, P * (t + 1)))
+        quantize(kt_mx, E4M3, HALF, N, kt_bf[1][:])
 
-        v_g = sb("v_g", [P, 2 * N], BF16)
-        v_bf = sb("v_bf", [P, N * PACK], BF16)
-        v_places = v_bf[:].rearrange("p (c j) -> p c j", j=PACK)
-        a_slots = sb("a_slots", [P, PACK, R], F32)
-        a_banks = [bank("turn") for t in range(PACK)]
-        for s in range(PACK):
-            scores = bank("mm")
-            matmul(scores[:], k_mx, E4M3, s, q_mx, E4M3)
-            nc.scalar.activation(
-                a_slots[:, s, :].rearrange("p (t m) -> p t m", t=PACK),
-                scores[:].rearrange("p (m t) -> p t m", t=PACK),
-                ACT.Copy,
-                scale=ts_col[:, s : s + 1],
-            )
-        for s in range(PACK):
-            for t in range(PACK):
-                nc.tensor.transpose(
-                    a_banks[t][:, P * s : P * (s + 1)], a_slots[:, s, P * t : P * (t + 1)], ident[:]
-                )
+        a_sb = [sb("a_sb%d" % t, [P, N], F32) for t in range(PACK)]
         p_sb = [sb("p_sb%d" % t, [P, N], F32) for t in range(PACK)]
         for t in range(PACK):
-            nc.scalar.activation(p_sb[t][:], a_banks[t][:], ACT.Exp, bias=neg_lse[:, t : t + 1])
+            scores = bank("mm")
+            matmul(scores[:], q_mx, E4M3, t, k_mx, E4M3)
+            nc.vector.tensor_tensor(a_sb[t][:], scores[:], ts_row[:], ALU.mult)
+            nc.scalar.activation(p_sb[t][:], a_sb[t][:], ACT.Exp, bias=neg_lse[:, t : t + 1])
 
-        def weigh(w, t):
-            nc.vector.scalar_tensor_tensor(w, p_sb[t][:], rw_c[:, t : t + 1], ts_row[:], ALU.mult, ALU.mult)
-
+        v_bf = sb("v_bf", [P, N * PACK], BF16, "q_bf")
+        v_places = v_bf[:].rearrange("p (c j) -> p c j", j=PACK)
         gather(v_places[:, :, 0], v_pool[0])
-        kt_mx = mx_tiles("kt", "v_pool0")
-        for h in range(2):
-            quantize(kt_mx, E4M3, HALF * h, HALF * (h + 1), kt_bf[h][:])
         gather(v_places[:, :, 1], v_pool[1])
-        gather(v_g[:, 0:N], v_pool[2])
-        w_pair = sb("w_pair", [P, 2 * N], F32, "v_pool2")
-        w_sb = [w_pair[:, 0:N], w_pair[:, N : 2 * N]]
+        w_pair = sb("w_pair", [P, 2 * N], F32, "v_pool1")
+        w_sb = {(t, c0): w_pair[:, N * t + c0 : N * t + c0 + HALF] for t in range(2) for c0 in (0, HALF)}
         for t in range(2):
-            weigh(w_sb[t], t)
-        w_last = sb("w_last", [P, N], F32, "p_sb1")
-        nc.gpsimd.tensor_tensor(w_last[:], p_sb[PACK - 1][:], ts_rw[:], ALU.mult)
+            nc.vector.scalar_tensor_tensor(
+                w_pair[:, N * t : N * (t + 1)], p_sb[t][:], rw_c[:, t : t + 1], ts_row[:], ALU.mult, ALU.mult
+            )
+        for t in range(2, PACK):
+            for c0 in (0, HALF):
+                w_sb[t, c0] = sb("w%d_%d" % (t, c0), [P, HALF], F32)[:]
+                first = N * (t - 2) + c0
+                nc.gpsimd.tensor_tensor(w_sb[t, c0], p_sb[t][:, c0 : c0 + HALF], ts_rw[:, first : first + HALF], ALU.mult)
+        v_g = sb("v_g", [P, 2 * N], BF16, "neg_lse")
+        gather_on_scalar(v_g[:, 0:N], v_pool[2])
         v_mx = mx_tiles("v")
-        for c0 in (0, HALF):
-            gather(v_g[:, N + c0 : N + c0 + HALF], v_pool[3], c0, c0 + HALF)
+        gather(v_g[:, N : N + HALF], v_pool[3], 0, HALF)
+        gather_on_scalar(v_g[:, N + HALF : 2 * N], v_pool[3], HALF, N)
         for c0 in (0, HALF):
             nc.vector.tensor_copy(*pair_views(v_bf, v_g, 1, c0, c0 + HALF))
         for c0 in (0, HALF):
@@ -221,17 +217,17 @@ def tile_attend_gat_lse_qk_ts_kernel(
         do_mx = mx_tiles("do")
         for h in range(PACK):
             nc.scalar.copy(*query_views(do_bf, do_raw[h][:], P // PACK * h, P // PACK * (h + 1)))
-        w_third = sb("w_third", [P, N], F32, "v_pool3")
-        weigh(w_third[:], 2)
-        w_sb.extend([w_third[:], w_last[:]])
         for t in range(PACK):
             quantize(do_mx, E5M2, P * t, P * (t + 1), laid(do_bf, P * t, P * (t + 1)))
 
-        qm_bf = sb("qm_bf", [P, D * PACK], BF16)
+        qm_bf = [sb("qm_bf%d" % b, [P, P * PACK], BF16) for b in range(PACK - 1)]
         qm_mx = mx_tiles("qm")
 
         def lay_qm(b):
-            nc.scalar.copy(*interleave_views(qm_bf, P * b, P * (b + 1), qm_raw[b][:]))
+            nc.scalar.copy(*interleave_views(qm_bf[b], 0, P, qm_raw[b][:]))
+
+        def quantize_qm(b):
+            quantize(qm_mx, E4M3, P * b, P * (b + 1), qm_bf[b][:])
 
         def quantize_block(mx, fmt, tile, b0, b1):
             quantize(mx, fmt, P * b0, P * b1, laid(tile, P * b0, P * b1))
@@ -246,7 +242,7 @@ def tile_attend_gat_lse_qk_ts_kernel(
                 ds_bf[:, N * t + c0 : N * t + c0 + HALF],
                 dp[t][:, c0 : c0 + HALF],
                 delta_c[:, t : t + 1],
-                w_sb[t][:, c0 : c0 + HALF],
+                w_sb[t, c0],
                 ALU.subtract,
                 ALU.mult,
             )
@@ -264,8 +260,8 @@ def tile_attend_gat_lse_qk_ts_kernel(
                 turned[:, 0 : 2 * P].rearrange("p (u m) -> p m u", u=2),
             )
 
-        dk_sb = [sb("dk_sb%d" % b, [P, N], F32) for b in range(PACK)]
-        gq_sb = [sb("gq_sb%d" % t, [P, D], F32) for t in range(2)]
+        dk_sb = [sb("dk_sb%d" % b, [P, N], F32) for b in range(2)]
+        gq_sb = [sb("gq_sb%d" % t, [P, D], F32) for t in range(PACK)]
         gq_rows = out_0[0].rearrange("(m t) d -> m t d", t=PACK)
 
         def key_gradient(copy, b, c0, c1):
@@ -301,9 +297,10 @@ def tile_attend_gat_lse_qk_ts_kernel(
         gradient(0, HALF)
         nc.vector.tensor_copy(*interleave_views(dsr_bf, 0, P, ds_planes[:, :, 0:P]))
         nc.scalar.copy(*interleave_views(dsr_bf, P, HALF, ds_planes[:, :, P:HALF]))
+        qm_bf.append(sb("qm_bf3", [P, P * PACK], BF16, "w3_0"))
         lay_qm(PACK - 1)
         gradient(1, HALF)
-        quantize_block(qm_mx, E4M3, qm_bf, 0, 1)
+        quantize_qm(0)
         quantize_block(dsr_mx, E5M2, dsr_bf, 0, 2)
         gradient(2, HALF)
         gradient(3, HALF)
@@ -315,26 +312,26 @@ def tile_attend_gat_lse_qk_ts_kernel(
         scatter_on_scalar(0, 0)
         quantize_block(dss_mx, E5M2, dss_bf, 0, 2)
         nc.vector.tensor_copy(*interleave_views(dsr_bf, HALF, N, ds_planes[:, :, HALF:N]))
-        quantize_block(qm_mx, E4M3, qm_bf, 1, 2)
+        quantize_qm(1)
         quantize_block(dsr_mx, E5M2, dsr_bf, 2, 4)
         query_gradient(nc.vector.tensor_copy, 0)
         key_gradient(nc.vector.tensor_copy, 0, HALF, N)
         scatter_on_scalar(0, HALF)
         store_window(0)
         quantize_block(dss_mx, E5M2, dss_bf, 2, 4)
-        query_gradient(nc.vector.tensor_copy, 1)
-        quantize_block(qm_mx, E4M3, qm_bf, 2, 4)
+        for t in range(1, PACK):
+            query_gradient(nc.vector.tensor_copy, t)
+        quantize_qm(2)
+        quantize_qm(3)
         key_gradient(nc.vector.tensor_copy, 1, 0, N)
         scatter_on_vector(1)
         store_window(1)
+        dk_late = sb("dk_late", [P, 2 * N], F32, "dk_sb0")
+        dk_sb.extend([dk_late[:, 0:N], dk_late[:, N : 2 * N]])
         key_gradient(nc.scalar.copy, 2, 0, N)
+        key_gradient(nc.scalar.copy, 3, 0, N)
         for c0 in (0, HALF):
             scatter_on_scalar(2, c0)
         store_window(2)
-        gq_late = sb("gq_late", [P, 2 * D], F32, "dk_sb2")
-        gq_sb.extend([gq_late[:, 0:D], gq_late[:, D : 2 * D]])
-        for t in range(2, PACK):
-            query_gradient(nc.scalar.copy, t)
-        key_gradient(nc.vector.tensor_copy, 3, 0, N)
         scatter_on_vector(3)
         store_window(3)

@@ -22,7 +22,7 @@ WIDTH = 512
 HALF = WIDTH // 2
 BAND = 16
 RUN = 4
-Q_SPLIT = 48
+Q_SPLIT = 64
 BANKS_PER_TAG = 4
 
 
@@ -80,6 +80,8 @@ def tile_attend_gat_lse_qk_ts_kernel(
             return out, planes.rearrange("p j (m t) -> p m j t", t=PACK)
 
         offsets = keep.tile([P, N // BAND], U16, name="offsets")
+        lse_c = sb("lse_c", [P, PACK], F32)
+        nc.sync.dma_start(lse_c[:], lse[0].rearrange("(p t) o -> p (t o)", t=PACK))
         nc.sync.dma_start(offsets[:], offs)
         k_rows = kT.rearrange("(p j) t -> p j t", j=PACK)
         v_rows = vT.rearrange("(p j) t -> p j t", j=PACK)
@@ -91,15 +93,13 @@ def tile_attend_gat_lse_qk_ts_kernel(
         ts_pool = sb("ts_pool", [P, T], F32)
         nc.vector.memset(ts_pool[:], 0.0)
         windows = [sb("window%d" % b, [P, T], F32) for b in range(PACK)]
+        nc.vector.memset(windows[0][:], 0.0)
         ts_raw = sb("ts_raw", [1, T], F32)
         nc.sync.dma_start(ts_raw[:], ts[0:1, :])
-        nc.vector.tensor_copy(ts_pool[0:1, :], ts_raw[:])
-        lse_c = sb("lse_c", [P, PACK], F32)
         delta_c = sb("delta_c", [P, PACK], F32)
         rw_c = sb("rw_c", [P, PACK], F32)
         nc.sync.dma_start(k_pool[0][:], k_rows[:, 0, :])
-        for columns, vector in ((lse_c, lse), (rw_c, rw)):
-            nc.sync.dma_start(columns[:], vector[0].rearrange("(p t) o -> p (t o)", t=PACK))
+        nc.sync.dma_start(rw_c[:], rw[0].rearrange("(p t) o -> p (t o)", t=PACK))
         for j in range(1, PACK):
             nc.sync.dma_start(k_pool[j][:], k_rows[:, j, :])
         nc.sync.dma_start(q_raw[:], qT[0].rearrange("(p j) r -> p j r", j=PACK))
@@ -115,7 +115,7 @@ def tile_attend_gat_lse_qk_ts_kernel(
 
         ident = sb("ident", [P, P], F32)
         make_identity(nc, ident[:])
-        for window in windows:
+        for window in windows[1:]:
             nc.gpsimd.memset(window[:], 0.0)
 
         k_g = [sb("k_g%d" % h, [P, 2 * N], BF16) for h in range(2)]
@@ -140,6 +140,8 @@ def tile_attend_gat_lse_qk_ts_kernel(
 
         neg_lse = sb("neg_lse", [P, PACK], F32)
         nc.scalar.activation(neg_lse[:], lse_c[:], ACT.Copy, scale=-1.0)
+        nc.scalar.copy(ts_pool[0:1, :], ts_raw[:])
+        gather_plane(k_g, k_pool, 0)
 
         ts_g = sb("ts_g", [P, N], F32)
         gather(ts_g[:], ts_pool)
@@ -153,12 +155,8 @@ def tile_attend_gat_lse_qk_ts_kernel(
             nc.tensor.transpose(turned[:, P * s : P * (s + 1)], ts_col[:, s : s + 1].to_broadcast([P, P]), ident[:])
         ts_row = sb("ts_row", [P, N], F32)
         nc.scalar.copy(ts_row[:], turned[:])
-        ts_rw = sb("ts_rw", [P, 2 * N], F32)
-        for t in range(2, PACK):
-            nc.scalar.activation(ts_rw[:, N * (t - 2) : N * (t - 1)], turned[:], ACT.Copy, scale=rw_c[:, t : t + 1])
 
-        for j in range(2):
-            gather_plane(k_g, k_pool, j)
+        gather_plane(k_g, k_pool, 1)
         k_bf = sb("k_bf", [P, N * PACK], BF16)
         nc.vector.tensor_copy(*pair_views(k_bf, k_g[0], 0))
         turn_keys(0)
@@ -189,21 +187,22 @@ def tile_attend_gat_lse_qk_ts_kernel(
             nc.vector.tensor_tensor(a_sb[t][:], scores[:], ts_row[:], ALU.mult)
             nc.scalar.activation(p_sb[t][:], a_sb[t][:], ACT.Exp, bias=neg_lse[:, t : t + 1])
 
-        v_bf = sb("v_bf", [P, N * PACK], BF16, "q_bf")
-        v_places = v_bf[:].rearrange("p (c j) -> p c j", j=PACK)
-        gather(v_places[:, :, 0], v_pool[0])
-        gather(v_places[:, :, 1], v_pool[1])
-        w_pair = sb("w_pair", [P, 2 * N], F32, "v_pool1")
-        w_sb = {(t, c0): w_pair[:, N * t + c0 : N * t + c0 + HALF] for t in range(2) for c0 in (0, HALF)}
-        for t in range(2):
+        v_bf = sb("v_bf", [P, N * PACK], BF16, "k_bf")
+        v_first = sb("v_first", [P, 2 * N], BF16, "q_bf")
+        for j in range(2):
+            gather(v_first[:, N * j : N * j + HALF], v_pool[j], 0, HALF)
+            gather_on_scalar(v_first[:, N * j + HALF : N * (j + 1)], v_pool[j], HALF, N)
+        nc.vector.tensor_copy(*pair_views(v_bf, v_first, 0))
+        w_first = sb("w_first", [P, 3 * N], F32, "v_pool1")
+        w_sb = {(t, c0): w_first[:, N * t + c0 : N * t + c0 + HALF] for t in range(3) for c0 in (0, HALF)}
+        for t in range(3):
             nc.vector.scalar_tensor_tensor(
-                w_pair[:, N * t : N * (t + 1)], p_sb[t][:], rw_c[:, t : t + 1], ts_row[:], ALU.mult, ALU.mult
+                w_first[:, N * t : N * (t + 1)], p_sb[t][:], rw_c[:, t : t + 1], ts_row[:], ALU.mult, ALU.mult
             )
-        for t in range(2, PACK):
-            for c0 in (0, HALF):
-                w_sb[t, c0] = sb("w%d_%d" % (t, c0), [P, HALF], F32)[:]
-                first = N * (t - 2) + c0
-                nc.gpsimd.tensor_tensor(w_sb[t, c0], p_sb[t][:, c0 : c0 + HALF], ts_rw[:, first : first + HALF], ALU.mult)
+        for c0 in (0, HALF):
+            w_sb[3, c0] = sb("w3_%d" % c0, [P, HALF], F32)[:]
+            cols = slice(c0, c0 + HALF)
+            nc.vector.scalar_tensor_tensor(w_sb[3, c0], p_sb[3][:, cols], rw_c[:, 3:4], ts_row[:, cols], ALU.mult, ALU.mult)
         v_g = sb("v_g", [P, 2 * N], BF16, "neg_lse")
         gather_on_scalar(v_g[:, 0:N], v_pool[2])
         v_mx = mx_tiles("v")
@@ -260,12 +259,11 @@ def tile_attend_gat_lse_qk_ts_kernel(
                 turned[:, 0 : 2 * P].rearrange("p (u m) -> p m u", u=2),
             )
 
-        dk_sb = [sb("dk_sb%d" % b, [P, N], F32) for b in range(2)]
+        dk_sb = [sb("dk_sb%d" % b, [P, N], F32, "k_pool%d" % b) for b in range(PACK)]
         gq_sb = [sb("gq_sb%d" % t, [P, D], F32) for t in range(PACK)]
         gq_rows = out_0[0].rearrange("(m t) d -> m t d", t=PACK)
 
-        def key_gradient(copy, b, c0, c1):
-            dk = bank("mm")
+        def key_gradient(copy, b, c0, c1, dk):
             matmul(dk[:, c0:c1], qm_mx, E4M3, b, dsr_mx, E5M2, c0, c1)
             copy(dk_sb[b][:, c0:c1], dk[:, c0:c1])
 
@@ -306,7 +304,7 @@ def tile_attend_gat_lse_qk_ts_kernel(
         gradient(3, HALF)
         turn_gradient(0)
         turn_gradient(1)
-        key_gradient(nc.scalar.copy, 0, 0, HALF)
+        key_gradient(nc.scalar.copy, 0, 0, HALF, dp[0])
         turn_gradient(2)
         turn_gradient(3)
         scatter_on_scalar(0, 0)
@@ -314,8 +312,8 @@ def tile_attend_gat_lse_qk_ts_kernel(
         nc.vector.tensor_copy(*interleave_views(dsr_bf, HALF, N, ds_planes[:, :, HALF:N]))
         quantize_qm(1)
         quantize_block(dsr_mx, E5M2, dsr_bf, 2, 4)
-        query_gradient(nc.vector.tensor_copy, 0)
-        key_gradient(nc.vector.tensor_copy, 0, HALF, N)
+        query_gradient(nc.scalar.copy, 0)
+        key_gradient(nc.vector.tensor_copy, 0, HALF, N, dp[1])
         scatter_on_scalar(0, HALF)
         store_window(0)
         quantize_block(dss_mx, E5M2, dss_bf, 2, 4)
@@ -323,15 +321,13 @@ def tile_attend_gat_lse_qk_ts_kernel(
             query_gradient(nc.vector.tensor_copy, t)
         quantize_qm(2)
         quantize_qm(3)
-        key_gradient(nc.vector.tensor_copy, 1, 0, N)
+        key_gradient(nc.vector.tensor_copy, 1, 0, N, dp[2])
         scatter_on_vector(1)
         store_window(1)
-        dk_late = sb("dk_late", [P, 2 * N], F32, "dk_sb0")
-        dk_sb.extend([dk_late[:, 0:N], dk_late[:, N : 2 * N]])
-        key_gradient(nc.scalar.copy, 2, 0, N)
-        key_gradient(nc.scalar.copy, 3, 0, N)
+        key_gradient(nc.scalar.copy, 2, 0, N, dp[1])
         for c0 in (0, HALF):
             scatter_on_scalar(2, c0)
         store_window(2)
+        key_gradient(nc.vector.tensor_copy, 3, 0, N, dp[2])
         scatter_on_vector(3)
         store_window(3)

@@ -22,7 +22,6 @@ WIDTH = 512
 HALF = WIDTH // 2
 BAND = 16
 RUN = 4
-Q_SPLIT = 64
 BANKS_PER_TAG = 4
 
 
@@ -80,14 +79,11 @@ def tile_attend_gat_lse_qk_ts_kernel(
             return out, planes.rearrange("p j (m t) -> p m j t", t=PACK)
 
         offsets = keep.tile([P, N // BAND], U16, name="offsets")
-        lse_c = sb("lse_c", [P, PACK], F32)
-        nc.sync.dma_start(lse_c[:], lse[0].rearrange("(p t) o -> p (t o)", t=PACK))
-        nc.sync.dma_start(offsets[:], offs)
         k_rows = kT.rearrange("(p j) t -> p j t", j=PACK)
         v_rows = vT.rearrange("(p j) t -> p j t", j=PACK)
         k_pool = [sb("k_pool%d" % j, [P, T], F32) for j in range(PACK)]
         v_pool = [sb("v_pool%d" % j, [P, T], F32) for j in range(PACK)]
-        q_raw = sb("q_raw", [P, PACK, R], F32)
+        q_raw = [sb("q_raw%d" % h, [P, PACK, HALF], F32) for h in range(2)]
         do_raw = [sb("do_raw%d" % h, [P, PACK, P], F32) for h in range(PACK)]
         qm_raw = [sb("qm_raw%d" % b, [P, PACK, P], F32) for b in range(PACK)]
         ts_pool = sb("ts_pool", [P, T], F32)
@@ -95,14 +91,19 @@ def tile_attend_gat_lse_qk_ts_kernel(
         windows = [sb("window%d" % b, [P, T], F32) for b in range(PACK)]
         nc.vector.memset(windows[0][:], 0.0)
         ts_raw = sb("ts_raw", [1, T], F32)
-        nc.sync.dma_start(ts_raw[:], ts[0:1, :])
+        lse_c = sb("lse_c", [P, PACK], F32)
         delta_c = sb("delta_c", [P, PACK], F32)
         rw_c = sb("rw_c", [P, PACK], F32)
+        nc.sync.dma_start(lse_c[:], lse[0].rearrange("(p t) o -> p (t o)", t=PACK))
+        nc.sync.dma_start(ts_raw[:], ts[0:1, :])
         nc.sync.dma_start(k_pool[0][:], k_rows[:, 0, :])
+        nc.sync.dma_start(offsets[:], offs)
         nc.sync.dma_start(rw_c[:], rw[0].rearrange("(p t) o -> p (t o)", t=PACK))
         for j in range(1, PACK):
             nc.sync.dma_start(k_pool[j][:], k_rows[:, j, :])
-        nc.sync.dma_start(q_raw[:], qT[0].rearrange("(p j) r -> p j r", j=PACK))
+        q_rows = qT[0].rearrange("(p j) r -> p j r", j=PACK)
+        for h in range(2):
+            nc.sync.dma_start(q_raw[h][:], q_rows[:, :, HALF * h : HALF * (h + 1)])
         for j in range(PACK):
             nc.sync.dma_start(v_pool[j][:], v_rows[:, j, :])
         do_rows = doT[0].rearrange("(p j) r -> p j r", j=PACK)
@@ -168,15 +169,15 @@ def tile_attend_gat_lse_qk_ts_kernel(
         k_mx = mx_tiles("k")
         nc.vector.tensor_copy(*pair_views(k_bf, k_g[1], 1))
         quantize(k_mx, E4M3, 0, N, k_bf[:])
-        kt_bf.append(sb("kt_bf1", [P, HALF * PACK], BF16))
-        turn_keys(1)
-
         q_bf = sb("q_bf", [P, R * PACK], BF16)
         q_mx = mx_tiles("q")
-        nc.scalar.copy(*query_views(q_bf, q_raw[:, :, 0 : PACK * Q_SPLIT], 0, Q_SPLIT))
-        nc.vector.tensor_copy(*query_views(q_bf, q_raw[:, :, PACK * Q_SPLIT : R], Q_SPLIT, P))
+        nc.scalar.copy(*query_views(q_bf, q_raw[0][:], 0, P // 2))
+        nc.scalar.copy(*query_views(q_bf, q_raw[1][:, :, 0:P], P // 2, 3 * P // 4))
+        nc.vector.tensor_copy(*query_views(q_bf, q_raw[1][:, :, P:HALF], 3 * P // 4, P))
         for t in range(PACK):
             quantize(q_mx, E4M3, P * t, P * (t + 1), laid(q_bf, P * t, P * (t + 1)))
+        kt_bf.append(sb("kt_bf1", [P, HALF * PACK], BF16, "q_raw1"))
+        turn_keys(1)
         quantize(kt_mx, E4M3, HALF, N, kt_bf[1][:])
 
         a_sb = [sb("a_sb%d" % t, [P, N], F32) for t in range(PACK)]
@@ -188,12 +189,12 @@ def tile_attend_gat_lse_qk_ts_kernel(
             nc.scalar.activation(p_sb[t][:], a_sb[t][:], ACT.Exp, bias=neg_lse[:, t : t + 1])
 
         v_bf = sb("v_bf", [P, N * PACK], BF16, "k_bf")
-        v_first = sb("v_first", [P, 2 * N], BF16, "q_bf")
-        for j in range(2):
-            gather(v_first[:, N * j : N * j + HALF], v_pool[j], 0, HALF)
-            gather_on_scalar(v_first[:, N * j + HALF : N * (j + 1)], v_pool[j], HALF, N)
+        v_first = sb("v_first", [P, 2 * N], BF16)
+        gather_on_scalar(v_first[:, 0:N], v_pool[0])
+        gather(v_first[:, N : N + HALF], v_pool[1], 0, HALF)
+        gather_on_scalar(v_first[:, N + HALF : 2 * N], v_pool[1], HALF, N)
         nc.vector.tensor_copy(*pair_views(v_bf, v_first, 0))
-        w_first = sb("w_first", [P, 3 * N], F32, "v_pool1")
+        w_first = sb("w_first", [P, 3 * N], F32, "ts_raw")
         w_sb = {(t, c0): w_first[:, N * t + c0 : N * t + c0 + HALF] for t in range(3) for c0 in (0, HALF)}
         for t in range(3):
             nc.vector.scalar_tensor_tensor(

@@ -87,15 +87,15 @@ def tile_attend_gat_lse_qk_ts_kernel(
         do_raw = [sb("do_raw%d" % h, [P, PACK, P], F32) for h in range(PACK)]
         qm_raw = [sb("qm_raw%d" % b, [P, PACK, P], F32) for b in range(PACK)]
         ts_pool = sb("ts_pool", [P, T], F32)
-        nc.vector.memset(ts_pool[:], 0.0)
         windows = [sb("window%d" % b, [P, T], F32) for b in range(PACK)]
-        nc.vector.memset(windows[0][:], 0.0)
-        ts_raw = sb("ts_raw", [1, T], F32)
+        for window in windows[:-1]:
+            nc.vector.memset(window[:], 0.0)
+        ts_raw = sb("ts_raw", [P, T // P], F32)
         lse_c = sb("lse_c", [P, PACK], F32)
         delta_c = sb("delta_c", [P, PACK], F32)
         rw_c = sb("rw_c", [P, PACK], F32)
         nc.sync.dma_start(lse_c[:], lse[0].rearrange("(p t) o -> p (t o)", t=PACK))
-        nc.sync.dma_start(ts_raw[:], ts[0:1, :])
+        nc.sync.dma_start(ts_raw[:], ts[0].rearrange("(p c) -> p c", p=P))
         nc.sync.dma_start(k_pool[0][:], k_rows[:, 0, :])
         nc.sync.dma_start(offsets[:], offs)
         nc.sync.dma_start(rw_c[:], rw[0].rearrange("(p t) o -> p (t o)", t=PACK))
@@ -116,8 +116,7 @@ def tile_attend_gat_lse_qk_ts_kernel(
 
         ident = sb("ident", [P, P], F32)
         make_identity(nc, ident[:])
-        for window in windows[1:]:
-            nc.gpsimd.memset(window[:], 0.0)
+        nc.gpsimd.memset(windows[-1][:], 0.0)
 
         k_g = [sb("k_g%d" % h, [P, 2 * N], BF16) for h in range(2)]
         kt_bf = [sb("kt_bf0", [P, HALF * PACK], BF16)]
@@ -141,22 +140,17 @@ def tile_attend_gat_lse_qk_ts_kernel(
 
         neg_lse = sb("neg_lse", [P, PACK], F32)
         nc.scalar.activation(neg_lse[:], lse_c[:], ACT.Copy, scale=-1.0)
-        nc.scalar.copy(ts_pool[0:1, :], ts_raw[:])
+        ts_places = ts_pool[:].rearrange("m (p c) -> m p c", p=P)
+        for c0 in range(0, T // P, PACK):
+            turned = bank("turn")
+            for c in range(PACK):
+                column = ts_raw[:, c0 + c : c0 + c + 1].to_broadcast([P, P])
+                nc.tensor.transpose(turned[:, P * c : P * (c + 1)], column, ident[:])
+            nc.scalar.copy(ts_places[:, :, c0 : c0 + PACK], turned[:].rearrange("m (c p) -> m p c", c=PACK))
         gather_plane(k_g, k_pool, 0)
 
-        ts_g = sb("ts_g", [P, N], F32)
-        gather(ts_g[:], ts_pool)
-        turned = bank("turn")
-        for s in range(PACK):
-            nc.tensor.transpose(turned[:, P * s : P * (s + 1)], ts_g[:, P * s : P * (s + 1)], ident[:])
-        ts_col = sb("ts_col", [P, PACK], F32)
-        nc.scalar.copy(ts_col[:], turned[:, 0::P])
-        turned = bank("turn")
-        for s in range(PACK):
-            nc.tensor.transpose(turned[:, P * s : P * (s + 1)], ts_col[:, s : s + 1].to_broadcast([P, P]), ident[:])
         ts_row = sb("ts_row", [P, N], F32)
-        nc.scalar.copy(ts_row[:], turned[:])
-
+        gather_on_scalar(ts_row[:], ts_pool)
         gather_plane(k_g, k_pool, 1)
         k_bf = sb("k_bf", [P, N * PACK], BF16)
         nc.vector.tensor_copy(*pair_views(k_bf, k_g[0], 0))
@@ -194,16 +188,12 @@ def tile_attend_gat_lse_qk_ts_kernel(
         gather(v_first[:, N : N + HALF], v_pool[1], 0, HALF)
         gather_on_scalar(v_first[:, N + HALF : 2 * N], v_pool[1], HALF, N)
         nc.vector.tensor_copy(*pair_views(v_bf, v_first, 0))
-        w_first = sb("w_first", [P, 3 * N], F32, "ts_raw")
-        w_sb = {(t, c0): w_first[:, N * t + c0 : N * t + c0 + HALF] for t in range(3) for c0 in (0, HALF)}
-        for t in range(3):
+        w_first = sb("w_first", [P, PACK * N], F32, "ts_pool")
+        w_sb = {(t, c0): w_first[:, N * t + c0 : N * t + c0 + HALF] for t in range(PACK) for c0 in (0, HALF)}
+        for t in range(PACK):
             nc.vector.scalar_tensor_tensor(
                 w_first[:, N * t : N * (t + 1)], p_sb[t][:], rw_c[:, t : t + 1], ts_row[:], ALU.mult, ALU.mult
             )
-        for c0 in (0, HALF):
-            w_sb[3, c0] = sb("w3_%d" % c0, [P, HALF], F32)[:]
-            cols = slice(c0, c0 + HALF)
-            nc.vector.scalar_tensor_tensor(w_sb[3, c0], p_sb[3][:, cols], rw_c[:, 3:4], ts_row[:, cols], ALU.mult, ALU.mult)
         v_g = sb("v_g", [P, 2 * N], BF16, "neg_lse")
         gather_on_scalar(v_g[:, 0:N], v_pool[2])
         v_mx = mx_tiles("v")
@@ -220,7 +210,7 @@ def tile_attend_gat_lse_qk_ts_kernel(
         for t in range(PACK):
             quantize(do_mx, E5M2, P * t, P * (t + 1), laid(do_bf, P * t, P * (t + 1)))
 
-        qm_bf = [sb("qm_bf%d" % b, [P, P * PACK], BF16) for b in range(PACK - 1)]
+        qm_bf = [sb("qm_bf%d" % b, [P, P * PACK], BF16) for b in range(PACK)]
         qm_mx = mx_tiles("qm")
 
         def lay_qm(b):
@@ -280,8 +270,7 @@ def tile_attend_gat_lse_qk_ts_kernel(
         def store_window(b):
             nc.sync.dma_start(out_1[P * b : P * (b + 1), :], windows[b][:])
 
-        def query_gradient(copy, t):
-            gq = bank("turn")
+        def query_gradient(copy, t, gq):
             matmul(gq[:], dss_mx, E5M2, t, kt_mx, E4M3)
             copy(
                 gq_sb[t][:].rearrange("m (p j) -> m p j", j=PACK),
@@ -289,43 +278,42 @@ def tile_attend_gat_lse_qk_ts_kernel(
             )
             nc.scalar.dma_start(gq_rows[:, t, :], gq_sb[t][:])
 
-        for b in range(PACK - 1):
+        for b in range(PACK):
             lay_qm(b)
         for t in range(PACK):
             gradient(t, 0)
         gradient(0, HALF)
         nc.vector.tensor_copy(*interleave_views(dsr_bf, 0, P, ds_planes[:, :, 0:P]))
         nc.scalar.copy(*interleave_views(dsr_bf, P, HALF, ds_planes[:, :, P:HALF]))
-        qm_bf.append(sb("qm_bf3", [P, P * PACK], BF16, "w3_0"))
-        lay_qm(PACK - 1)
         gradient(1, HALF)
         quantize_qm(0)
         quantize_block(dsr_mx, E5M2, dsr_bf, 0, 2)
+        turn_gradient(0)
+        key_gradient(nc.scalar.copy, 0, 0, HALF, dp[0])
+        scatter_on_scalar(0, 0)
         gradient(2, HALF)
         gradient(3, HALF)
-        turn_gradient(0)
         turn_gradient(1)
-        key_gradient(nc.scalar.copy, 0, 0, HALF, dp[0])
         turn_gradient(2)
         turn_gradient(3)
-        scatter_on_scalar(0, 0)
         quantize_block(dss_mx, E5M2, dss_bf, 0, 2)
         nc.vector.tensor_copy(*interleave_views(dsr_bf, HALF, N, ds_planes[:, :, HALF:N]))
         quantize_qm(1)
         quantize_block(dsr_mx, E5M2, dsr_bf, 2, 4)
-        query_gradient(nc.scalar.copy, 0)
-        key_gradient(nc.vector.tensor_copy, 0, HALF, N, dp[1])
+        query_gradient(nc.vector.tensor_copy, 0, bank("turn"))
+        key_gradient(nc.scalar.copy, 0, HALF, N, dp[1])
         scatter_on_scalar(0, HALF)
         store_window(0)
         quantize_block(dss_mx, E5M2, dss_bf, 2, 4)
-        for t in range(1, PACK):
-            query_gradient(nc.vector.tensor_copy, t)
+        for t in range(1, PACK - 1):
+            query_gradient(nc.vector.tensor_copy, t, bank("turn"))
+        query_gradient(nc.scalar.copy, PACK - 1, dp[1])
         quantize_qm(2)
         quantize_qm(3)
         key_gradient(nc.vector.tensor_copy, 1, 0, N, dp[2])
         scatter_on_vector(1)
         store_window(1)
-        key_gradient(nc.scalar.copy, 2, 0, N, dp[1])
+        key_gradient(nc.scalar.copy, 2, 0, N, dp[0])
         for c0 in (0, HALF):
             scatter_on_scalar(2, c0)
         store_window(2)

@@ -94,11 +94,11 @@ def tile_attend_gat_lse_qk_ts_kernel(
         lse_c = sb("lse_c", [P, PACK], F32)
         delta_c = sb("delta_c", [P, PACK], F32)
         rw_c = sb("rw_c", [P, PACK], F32)
-        nc.sync.dma_start(lse_c[:], lse[0].rearrange("(p t) o -> p (t o)", t=PACK))
-        nc.sync.dma_start(ts_raw[:], ts[0].rearrange("(p c) -> p c", p=P))
         nc.sync.dma_start(k_pool[0][:], k_rows[:, 0, :])
         nc.sync.dma_start(offsets[:], offs)
-        nc.sync.dma_start(rw_c[:], rw[0].rearrange("(p t) o -> p (t o)", t=PACK))
+        nc.sync.dma_start(ts_raw[:], ts[0].rearrange("(p c) -> p c", p=P))
+        for columns, vector in ((lse_c, lse), (rw_c, rw)):
+            nc.sync.dma_start(columns[:], vector[0].rearrange("(p t) o -> p (t o)", t=PACK))
         for j in range(1, PACK):
             nc.sync.dma_start(k_pool[j][:], k_rows[:, j, :])
         q_rows = qT[0].rearrange("(p j) r -> p j r", j=PACK)
@@ -307,13 +307,13 @@ def tile_attend_gat_lse_qk_ts_kernel(
         quantize_block(dss_mx, E5M2, dss_bf, 2, 4)
         for t in range(1, PACK - 1):
             query_gradient(nc.vector.tensor_copy, t, bank("turn"))
-        query_gradient(nc.scalar.copy, PACK - 1, dp[1])
         quantize_qm(2)
         quantize_qm(3)
         key_gradient(nc.vector.tensor_copy, 1, 0, N, dp[2])
         scatter_on_vector(1)
         store_window(1)
-        key_gradient(nc.scalar.copy, 2, 0, N, dp[0])
+        key_gradient(nc.scalar.copy, 2, 0, N, dp[1])
+        query_gradient(nc.scalar.copy, PACK - 1, dp[3])
         for c0 in (0, HALF):
             scatter_on_scalar(2, c0)
         store_window(2)

@@ -22,6 +22,7 @@ WIDTH = 512
 HALF = WIDTH // 2
 BAND = 16
 RUN = 4
+QUARTER = P // PACK
 BANKS_PER_TAG = 4
 
 
@@ -60,7 +61,7 @@ def tile_attend_gat_lse_qk_ts_kernel(
                 stop=True,
             )
 
-        def gather(out, window, c0=0, c1=N):
+        def gather_on_vector(out, window, c0=0, c1=N):
             nc.vector.tensor_copy(out, window[:].indirect(offsets[:, c0 // BAND : c1 // BAND]))
 
         def gather_on_scalar(out, window, c0=0, c1=N):
@@ -74,9 +75,9 @@ def tile_attend_gat_lse_qk_ts_kernel(
             out = dst[:].rearrange("p (c j) -> p c j", j=PACK)[:, c0:c1, 2 * h : 2 * h + 2]
             return out, pair[:].rearrange("p (j c) -> p c j", j=2)[:, c0:c1]
 
-        def query_views(dst, planes, m0, m1):
-            out = dst[:].rearrange("p (t m j) -> p m j t", t=PACK, j=PACK)[:, m0:m1]
-            return out, planes.rearrange("p j (m t) -> p m j t", t=PACK)
+        def query_views(dst, planes, m0, m1, t0=0, t1=PACK):
+            out = dst[:].rearrange("p (t m j) -> p m j t", t=PACK, j=PACK)[:, m0:m1, :, t0:t1]
+            return out, planes.rearrange("p j (m t) -> p m j t", t=PACK)[:, :, :, t0:t1]
 
         offsets = keep.tile([P, N // BAND], U16, name="offsets")
         k_rows = kT.rearrange("(p j) t -> p j t", j=PACK)
@@ -135,8 +136,8 @@ def tile_attend_gat_lse_qk_ts_kernel(
                 turned[:].rearrange("m (e u p) -> m e p u", e=2, u=2),
             )
 
-        def gather_plane(pairs, pool, j):
-            gather(pairs[j // 2][:, N * (j % 2) : N * (j % 2 + 1)], pool[j])
+        def gather_key_plane(j):
+            gather_on_vector(k_g[j // 2][:, N * (j % 2) : N * (j % 2 + 1)], k_pool[j])
 
         neg_lse = sb("neg_lse", [P, PACK], F32)
         nc.scalar.activation(neg_lse[:], lse_c[:], ACT.Copy, scale=-1.0)
@@ -147,27 +148,27 @@ def tile_attend_gat_lse_qk_ts_kernel(
                 column = ts_raw[:, c0 + c : c0 + c + 1].to_broadcast([P, P])
                 nc.tensor.transpose(turned[:, P * c : P * (c + 1)], column, ident[:])
             nc.scalar.copy(ts_places[:, :, c0 : c0 + PACK], turned[:].rearrange("m (c p) -> m p c", c=PACK))
-        gather_plane(k_g, k_pool, 0)
-
+        gather_key_plane(0)
         ts_row = sb("ts_row", [P, N], F32)
         gather_on_scalar(ts_row[:], ts_pool)
-        gather_plane(k_g, k_pool, 1)
+        gather_key_plane(1)
         k_bf = sb("k_bf", [P, N * PACK], BF16)
         nc.vector.tensor_copy(*pair_views(k_bf, k_g[0], 0))
         turn_keys(0)
         kt_mx = mx_tiles("kt")
-        gather_plane(k_g, k_pool, 2)
+        gather_key_plane(2)
         quantize(kt_mx, E4M3, 0, HALF, kt_bf[0][:])
-        gather(k_g[1][:, N : N + HALF], k_pool[3], 0, HALF)
+        gather_on_vector(k_g[1][:, N : N + HALF], k_pool[3], 0, HALF)
         gather_on_scalar(k_g[1][:, N + HALF : 2 * N], k_pool[3], HALF, N)
         k_mx = mx_tiles("k")
         nc.vector.tensor_copy(*pair_views(k_bf, k_g[1], 1))
         quantize(k_mx, E4M3, 0, N, k_bf[:])
+
         q_bf = sb("q_bf", [P, R * PACK], BF16)
         q_mx = mx_tiles("q")
-        nc.scalar.copy(*query_views(q_bf, q_raw[0][:], 0, P // 2))
-        nc.scalar.copy(*query_views(q_bf, q_raw[1][:, :, 0:P], P // 2, 3 * P // 4))
-        nc.vector.tensor_copy(*query_views(q_bf, q_raw[1][:, :, P:HALF], 3 * P // 4, P))
+        nc.scalar.copy(*query_views(q_bf, q_raw[0][:], 0, 2 * QUARTER))
+        nc.scalar.copy(*query_views(q_bf, q_raw[1][:, :, 0:P], 2 * QUARTER, 3 * QUARTER))
+        nc.vector.tensor_copy(*query_views(q_bf, q_raw[1][:, :, P:HALF], 3 * QUARTER, P))
         for t in range(PACK):
             quantize(q_mx, E4M3, P * t, P * (t + 1), laid(q_bf, P * t, P * (t + 1)))
         kt_bf.append(sb("kt_bf1", [P, HALF * PACK], BF16, "q_raw1"))
@@ -185,28 +186,31 @@ def tile_attend_gat_lse_qk_ts_kernel(
         v_bf = sb("v_bf", [P, N * PACK], BF16, "k_bf")
         v_first = sb("v_first", [P, 2 * N], BF16)
         gather_on_scalar(v_first[:, 0:N], v_pool[0])
-        gather(v_first[:, N : N + HALF], v_pool[1], 0, HALF)
+        gather_on_vector(v_first[:, N : N + HALF], v_pool[1], 0, HALF)
         gather_on_scalar(v_first[:, N + HALF : 2 * N], v_pool[1], HALF, N)
         nc.vector.tensor_copy(*pair_views(v_bf, v_first, 0))
-        w_first = sb("w_first", [P, PACK * N], F32, "ts_pool")
-        w_sb = {(t, c0): w_first[:, N * t + c0 : N * t + c0 + HALF] for t in range(PACK) for c0 in (0, HALF)}
+        w_sb = sb("w_sb", [P, PACK * N], F32, "ts_pool")
         for t in range(PACK):
             nc.vector.scalar_tensor_tensor(
-                w_first[:, N * t : N * (t + 1)], p_sb[t][:], rw_c[:, t : t + 1], ts_row[:], ALU.mult, ALU.mult
+                w_sb[:, N * t : N * (t + 1)], p_sb[t][:], rw_c[:, t : t + 1], ts_row[:], ALU.mult, ALU.mult
             )
         v_g = sb("v_g", [P, 2 * N], BF16, "neg_lse")
         gather_on_scalar(v_g[:, 0:N], v_pool[2])
         v_mx = mx_tiles("v")
-        gather(v_g[:, N : N + HALF], v_pool[3], 0, HALF)
+        gather_on_vector(v_g[:, N : N + HALF], v_pool[3], 0, HALF)
         gather_on_scalar(v_g[:, N + HALF : 2 * N], v_pool[3], HALF, N)
         for c0 in (0, HALF):
             nc.vector.tensor_copy(*pair_views(v_bf, v_g, 1, c0, c0 + HALF))
         for c0 in (0, HALF):
             quantize(v_mx, E4M3, c0, c0 + HALF, laid(v_bf, c0, c0 + HALF))
+
         do_bf = sb("do_bf", [P, R * PACK], BF16)
         do_mx = mx_tiles("do")
-        for h in range(PACK):
-            nc.scalar.copy(*query_views(do_bf, do_raw[h][:], P // PACK * h, P // PACK * (h + 1)))
+        for h in range(2):
+            nc.scalar.copy(*query_views(do_bf, do_raw[h][:], QUARTER * h, QUARTER * (h + 1)))
+        for t0 in (0, 2):
+            for h in range(2, PACK):
+                nc.scalar.copy(*query_views(do_bf, do_raw[h][:], QUARTER * h, QUARTER * (h + 1), t0, t0 + 2))
         for t in range(PACK):
             quantize(do_mx, E5M2, P * t, P * (t + 1), laid(do_bf, P * t, P * (t + 1)))
 
@@ -232,7 +236,7 @@ def tile_attend_gat_lse_qk_ts_kernel(
                 ds_bf[:, N * t + c0 : N * t + c0 + HALF],
                 dp[t][:, c0 : c0 + HALF],
                 delta_c[:, t : t + 1],
-                w_sb[t, c0],
+                w_sb[:, N * t + c0 : N * t + c0 + HALF],
                 ALU.subtract,
                 ALU.mult,
             )
@@ -282,14 +286,15 @@ def tile_attend_gat_lse_qk_ts_kernel(
             lay_qm(b)
         for t in range(PACK):
             gradient(t, 0)
-        gradient(0, HALF)
+        quantize_qm(0)
         nc.vector.tensor_copy(*interleave_views(dsr_bf, 0, P, ds_planes[:, :, 0:P]))
         nc.scalar.copy(*interleave_views(dsr_bf, P, HALF, ds_planes[:, :, P:HALF]))
+        quantize_block(dsr_mx, E5M2, dsr_bf, 0, 1)
+        quantize_block(dsr_mx, E5M2, dsr_bf, 1, 2)
+        gradient(0, HALF)
         gradient(1, HALF)
-        quantize_qm(0)
-        quantize_block(dsr_mx, E5M2, dsr_bf, 0, 2)
-        turn_gradient(0)
         key_gradient(nc.scalar.copy, 0, 0, HALF, dp[0])
+        turn_gradient(0)
         scatter_on_scalar(0, 0)
         gradient(2, HALF)
         gradient(3, HALF)

@@ -62,10 +62,10 @@ def tile_attend_gat_lse_qk_ts_kernel(
             )
 
         def gather_on_vector(out, window, c0=0, c1=N):
-            nc.vector.tensor_copy(out, window[:].indirect(offsets[:, c0 // BAND : c1 // BAND]))
+            nc.vector.tensor_copy(out, window.indirect(offsets[:, c0 // BAND : c1 // BAND]))
 
         def gather_on_scalar(out, window, c0=0, c1=N):
-            nc.scalar.activation(out, window[:].indirect(offsets[:, c0 // BAND : c1 // BAND]), ACT.Copy)
+            nc.scalar.activation(out, window.indirect(offsets[:, c0 // BAND : c1 // BAND]), ACT.Copy)
 
         def interleave_views(dst, c0, c1, planes):
             out = laid(dst, c0, c1).rearrange("p (c i j) -> p c j i", i=RUN, j=PACK)
@@ -82,9 +82,10 @@ def tile_attend_gat_lse_qk_ts_kernel(
         offsets = keep.tile([P, N // BAND], U16, name="offsets")
         k_rows = kT.rearrange("(p j) t -> p j t", j=PACK)
         v_rows = vT.rearrange("(p j) t -> p j t", j=PACK)
-        k_pool = [sb("k_pool%d" % j, [P, T], F32) for j in range(PACK)]
-        v_pool = [sb("v_pool%d" % j, [P, T], F32) for j in range(PACK)]
-        q_raw = [sb("q_raw%d" % h, [P, PACK, HALF], F32) for h in range(2)]
+        k_pair = sb("k_pair", [P, 2 * T], F32)
+        k_pool = [k_pair[:, 0:T], k_pair[:, T : 2 * T]] + [sb("k_pool%d" % j, [P, T], F32)[:] for j in (2, 3)]
+        v_pool = [sb("v_pool%d" % j, [P, T], F32)[:] for j in range(PACK)]
+        q_raw = sb("q_raw", [P, PACK, R], F32)
         do_raw = [sb("do_raw%d" % h, [P, PACK, P], F32) for h in range(PACK)]
         qm_raw = [sb("qm_raw%d" % b, [P, PACK, P], F32) for b in range(PACK)]
         ts_pool = sb("ts_pool", [P, T], F32)
@@ -95,18 +96,16 @@ def tile_attend_gat_lse_qk_ts_kernel(
         lse_c = sb("lse_c", [P, PACK], F32)
         delta_c = sb("delta_c", [P, PACK], F32)
         rw_c = sb("rw_c", [P, PACK], F32)
-        nc.sync.dma_start(k_pool[0][:], k_rows[:, 0, :])
-        nc.sync.dma_start(offsets[:], offs)
-        nc.sync.dma_start(ts_raw[:], ts[0].rearrange("(p c) -> p c", p=P))
+        nc.scalar.dma_start(ts_raw[:], ts[0].rearrange("(p c) -> p c", p=P))
         for columns, vector in ((lse_c, lse), (rw_c, rw)):
-            nc.sync.dma_start(columns[:], vector[0].rearrange("(p t) o -> p (t o)", t=PACK))
-        for j in range(1, PACK):
-            nc.sync.dma_start(k_pool[j][:], k_rows[:, j, :])
-        q_rows = qT[0].rearrange("(p j) r -> p j r", j=PACK)
-        for h in range(2):
-            nc.sync.dma_start(q_raw[h][:], q_rows[:, :, HALF * h : HALF * (h + 1)])
+            nc.scalar.dma_start(columns[:], vector[0].rearrange("(p t) o -> p (t o)", t=PACK))
+        nc.sync.dma_start(offsets[:], offs)
+        nc.sync.dma_start(k_pair[:].rearrange("p (j t) -> p j t", j=2), k_rows[:, 0:2, :])
+        for j in (2, 3):
+            nc.sync.dma_start(k_pool[j], k_rows[:, j, :])
+        nc.sync.dma_start(q_raw[:], qT[0].rearrange("(p j) r -> p j r", j=PACK))
         for j in range(PACK):
-            nc.sync.dma_start(v_pool[j][:], v_rows[:, j, :])
+            nc.sync.dma_start(v_pool[j], v_rows[:, j, :])
         do_rows = doT[0].rearrange("(p j) r -> p j r", j=PACK)
         for h in range(PACK):
             nc.sync.dma_start(do_raw[h][:], do_rows[:, :, P * h : P * (h + 1)])
@@ -120,27 +119,28 @@ def tile_attend_gat_lse_qk_ts_kernel(
         nc.gpsimd.memset(windows[-1][:], 0.0)
 
         k_g = [sb("k_g%d" % h, [P, 2 * N], BF16) for h in range(2)]
-        kt_bf = [sb("kt_bf0", [P, HALF * PACK], BF16)]
+        kt_bf = sb("kt_bf", [P, D * PACK], BF16)
 
-        def turn_pairs(turned, column, plane):
+        def turn_pairs(turned, column, plane, dealt=False):
             words = plane.bitcast(F32)
             for u in range(2):
-                nc.tensor.transpose(turned[:, column + P * u : column + P * (u + 1)], words[:, u::2], ident[:])
+                picked = words[:, P * u : P * (u + 1)] if dealt else words[:, u::2]
+                nc.tensor.transpose(turned[:, column + P * u : column + P * (u + 1)], picked, ident[:])
 
         def turn_keys(h):
             turned = bank("turn")
             for e in range(2):
-                turn_pairs(turned, HALF * e, k_g[h][:, N * e : N * (e + 1)])
+                turn_pairs(turned, HALF * e, k_g[h][:, N * e : N * (e + 1)], dealt=h == 0)
             nc.scalar.copy(
-                kt_bf[h][:].bitcast(F32).rearrange("m (e p u) -> m e p u", e=2, u=2),
+                laid(kt_bf, HALF * h, HALF * (h + 1)).bitcast(F32).rearrange("m (e p u) -> m e p u", e=2, u=2),
                 turned[:].rearrange("m (e u p) -> m e p u", e=2, u=2),
             )
 
-        def gather_key_plane(j):
-            gather_on_vector(k_g[j // 2][:, N * (j % 2) : N * (j % 2 + 1)], k_pool[j])
+        def gather_dealt_plane(j):
+            gather_on_vector(k_g[0][:, N * j : N * (j + 1)].rearrange("p (u m e) -> p m u e", u=2, e=2), k_pool[j])
 
         neg_lse = sb("neg_lse", [P, PACK], F32)
-        nc.scalar.activation(neg_lse[:], lse_c[:], ACT.Copy, scale=-1.0)
+        nc.vector.tensor_scalar(neg_lse[:], lse_c[:], -1.0, None, ALU.mult)
         ts_places = ts_pool[:].rearrange("m (p c) -> m p c", p=P)
         for c0 in range(0, T // P, PACK):
             turned = bank("turn")
@@ -148,32 +148,33 @@ def tile_attend_gat_lse_qk_ts_kernel(
                 column = ts_raw[:, c0 + c : c0 + c + 1].to_broadcast([P, P])
                 nc.tensor.transpose(turned[:, P * c : P * (c + 1)], column, ident[:])
             nc.scalar.copy(ts_places[:, :, c0 : c0 + PACK], turned[:].rearrange("m (c p) -> m p c", c=PACK))
-        gather_key_plane(0)
         ts_row = sb("ts_row", [P, N], F32)
-        gather_on_scalar(ts_row[:], ts_pool)
-        gather_key_plane(1)
-        k_bf = sb("k_bf", [P, N * PACK], BF16)
-        nc.vector.tensor_copy(*pair_views(k_bf, k_g[0], 0))
+        gather_on_scalar(ts_row[:], ts_pool[:])
+        gather_dealt_plane(0)
+        gather_dealt_plane(1)
         turn_keys(0)
-        kt_mx = mx_tiles("kt")
-        gather_key_plane(2)
-        quantize(kt_mx, E4M3, 0, HALF, kt_bf[0][:])
+        k_bf = sb("k_bf", [P, N * PACK], BF16)
+        nc.vector.tensor_copy(
+            k_bf[:].rearrange("p (m u e j) -> p m u e j", u=2, e=2, j=PACK)[:, :, :, :, 0:2],
+            k_g[0][:].rearrange("p (j u m e) -> p m u e j", j=2, u=2, e=2),
+        )
+        gather_on_vector(k_g[1][:, 0:N], k_pool[2])
         gather_on_vector(k_g[1][:, N : N + HALF], k_pool[3], 0, HALF)
         gather_on_scalar(k_g[1][:, N + HALF : 2 * N], k_pool[3], HALF, N)
+        turn_keys(1)
         k_mx = mx_tiles("k")
         nc.vector.tensor_copy(*pair_views(k_bf, k_g[1], 1))
         quantize(k_mx, E4M3, 0, N, k_bf[:])
+        kt_mx = mx_tiles("kt")
+        quantize(kt_mx, E4M3, 0, D, kt_bf[:])
 
-        q_bf = sb("q_bf", [P, R * PACK], BF16)
+        q_bf = [sb("q_bf%d" % h, [P, HALF * PACK], BF16) for h in range(2)]
         q_mx = mx_tiles("q")
-        nc.scalar.copy(*query_views(q_bf, q_raw[0][:], 0, 2 * QUARTER))
-        nc.scalar.copy(*query_views(q_bf, q_raw[1][:, :, 0:P], 2 * QUARTER, 3 * QUARTER))
-        nc.vector.tensor_copy(*query_views(q_bf, q_raw[1][:, :, P:HALF], 3 * QUARTER, P))
+        q_blocks = q_raw[:].rearrange("p j (m t) -> p m j t", t=PACK)
+        for h in range(2):
+            nc.scalar.copy(q_bf[h][:].rearrange("p (t m j) -> p m j t", t=2, j=PACK), q_blocks[:, :, :, 2 * h : 2 * h + 2])
         for t in range(PACK):
-            quantize(q_mx, E4M3, P * t, P * (t + 1), laid(q_bf, P * t, P * (t + 1)))
-        kt_bf.append(sb("kt_bf1", [P, HALF * PACK], BF16, "q_raw1"))
-        turn_keys(1)
-        quantize(kt_mx, E4M3, HALF, N, kt_bf[1][:])
+            quantize(q_mx, E4M3, P * t, P * (t + 1), laid(q_bf[t // 2], P * (t % 2), P * (t % 2 + 1)))
 
         a_sb = [sb("a_sb%d" % t, [P, N], F32) for t in range(PACK)]
         p_sb = [sb("p_sb%d" % t, [P, N], F32) for t in range(PACK)]
@@ -254,7 +255,7 @@ def tile_attend_gat_lse_qk_ts_kernel(
                 turned[:, 0 : 2 * P].rearrange("p (u m) -> p m u", u=2),
             )
 
-        dk_sb = [sb("dk_sb%d" % b, [P, N], F32, "k_pool%d" % b) for b in range(PACK)]
+        dk_sb = [sb("dk_sb%d" % b, [P, N], F32) for b in range(PACK)]
         gq_sb = [sb("gq_sb%d" % t, [P, D], F32) for t in range(PACK)]
         gq_rows = out_0[0].rearrange("(m t) d -> m t d", t=PACK)
 

@@ -215,7 +215,7 @@ def tile_attend_gat_lse_qk_ts_kernel(
         for t in range(PACK):
             quantize(do_mx, E5M2, P * t, P * (t + 1), laid(do_bf, P * t, P * (t + 1)))
 
-        qm_bf = [sb("qm_bf%d" % b, [P, P * PACK], BF16) for b in range(PACK)]
+        qm_bf = [sb("qm_bf%d" % b, [P, P * PACK], BF16, "do_bf" if b == 1 else None) for b in range(PACK)]
         qm_mx = mx_tiles("qm")
 
         def lay_qm(b):
@@ -283,8 +283,9 @@ def tile_attend_gat_lse_qk_ts_kernel(
             )
             nc.scalar.dma_start(gq_rows[:, t, :], gq_sb[t][:])
 
-        for b in range(PACK):
+        for b in (0, 2, 3):
             lay_qm(b)
+        nc.gpsimd.tensor_scalar(*interleave_views(qm_bf[1], 0, P, qm_raw[1][:]), 1.0, 0.0, ALU.mult, ALU.add)
         for t in range(PACK):
             gradient(t, 0)
         quantize_qm(0)

@@ -312,11 +312,11 @@ def tile_attend_gat_lse_qk_ts_kernel(
         scatter_on_scalar(0, HALF)
         store_window(0)
         quantize_block(dss_mx, E5M2, dss_bf, 2, 4)
-        for t in range(1, PACK - 1):
-            query_gradient(nc.vector.tensor_copy, t, bank("turn"))
+        query_gradient(nc.vector.tensor_copy, 1, bank("turn"))
         quantize_qm(2)
         quantize_qm(3)
         key_gradient(nc.vector.tensor_copy, 1, 0, N, dp[2])
+        query_gradient(nc.vector.tensor_copy, 2, bank("turn"))
         scatter_on_vector(1)
         store_window(1)
         key_gradient(nc.scalar.copy, 2, 0, N, dp[1])

@@ -23,7 +23,7 @@ HALF = WIDTH // 2
 BAND = 16
 RUN = 4
 QUARTER = P // PACK
-BANKS_PER_TAG = 4
+TURN = 4
 
 
 def tile_attend_gat_lse_qk_ts_kernel(
@@ -32,13 +32,13 @@ def tile_attend_gat_lse_qk_ts_kernel(
     nc = tc.nc
     with ExitStack() as ctx:
         keep = ctx.enter_context(tc.tile_pool(name="keep", bufs=1))
-        psum = ctx.enter_context(tc.psum_pool(name="psum", bufs=BANKS_PER_TAG))
+        psum = ctx.enter_context(tc.psum_pool(name="psum", bufs=1))
 
         def sb(name, shape, dtype, reuse=None):
             return keep.tile(shape, dtype, name=name, tag=reuse or name, align_bytes=64)
 
-        def bank(tag):
-            return psum.tile([P, WIDTH], F32, name=tag, tag=tag)
+        def bank(n):
+            return psum.tile([P, WIDTH], F32, name="bank%d" % n, tag="bank%d" % n)
 
         def mx_tiles(name, reuse=None):
             return sb(name + "_codes", [P, WIDTH], U32, reuse), sb(name + "_scales", [P, WIDTH], U8)
@@ -118,7 +118,7 @@ def tile_attend_gat_lse_qk_ts_kernel(
         make_identity(nc, ident[:])
         nc.gpsimd.memset(windows[-1][:], 0.0)
 
-        k_g = [sb("k_g%d" % h, [P, 2 * N], BF16) for h in range(2)]
+        k_g = [sb("k_g%d" % h, [P, 2 * N], BF16, "ts_pool" if h == 1 else None) for h in range(2)]
         kt_bf = sb("kt_bf", [P, D * PACK], BF16)
 
         def turn_pairs(turned, column, plane, dealt=False):
@@ -128,7 +128,7 @@ def tile_attend_gat_lse_qk_ts_kernel(
                 nc.tensor.transpose(turned[:, column + P * u : column + P * (u + 1)], picked, ident[:])
 
         def turn_keys(h):
-            turned = bank("turn")
+            turned = bank(TURN + 3 - 3 * h)
             for e in range(2):
                 turn_pairs(turned, HALF * e, k_g[h][:, N * e : N * (e + 1)], dealt=h == 0)
             nc.scalar.copy(
@@ -143,7 +143,7 @@ def tile_attend_gat_lse_qk_ts_kernel(
         nc.vector.tensor_scalar(neg_lse[:], lse_c[:], -1.0, None, ALU.mult)
         ts_places = ts_pool[:].rearrange("m (p c) -> m p c", p=P)
         for c0 in range(0, T // P, PACK):
-            turned = bank("turn")
+            turned = bank(TURN + c0 // PACK)
             for c in range(PACK):
                 column = ts_raw[:, c0 + c : c0 + c + 1].to_broadcast([P, P])
                 nc.tensor.transpose(turned[:, P * c : P * (c + 1)], column, ident[:])
@@ -168,24 +168,23 @@ def tile_attend_gat_lse_qk_ts_kernel(
         kt_mx = mx_tiles("kt")
         quantize(kt_mx, E4M3, 0, D, kt_bf[:])
 
-        q_bf = [sb("q_bf%d" % h, [P, HALF * PACK], BF16) for h in range(2)]
+        q_bf = sb("q_bf", [P, R * PACK], BF16, "k_g0")
         q_mx = mx_tiles("q")
-        q_blocks = q_raw[:].rearrange("p j (m t) -> p m j t", t=PACK)
         for h in range(2):
-            nc.scalar.copy(q_bf[h][:].rearrange("p (t m j) -> p m j t", t=2, j=PACK), q_blocks[:, :, :, 2 * h : 2 * h + 2])
+            nc.scalar.copy(*query_views(q_bf, q_raw[:], 0, P, 2 * h, 2 * h + 2))
         for t in range(PACK):
-            quantize(q_mx, E4M3, P * t, P * (t + 1), laid(q_bf[t // 2], P * (t % 2), P * (t % 2 + 1)))
+            quantize(q_mx, E4M3, P * t, P * (t + 1), laid(q_bf, P * t, P * (t + 1)))
 
         a_sb = [sb("a_sb%d" % t, [P, N], F32) for t in range(PACK)]
         p_sb = [sb("p_sb%d" % t, [P, N], F32) for t in range(PACK)]
         for t in range(PACK):
-            scores = bank("mm")
+            scores = bank(t)
             matmul(scores[:], q_mx, E4M3, t, k_mx, E4M3)
             nc.vector.tensor_tensor(a_sb[t][:], scores[:], ts_row[:], ALU.mult)
             nc.scalar.activation(p_sb[t][:], a_sb[t][:], ACT.Exp, bias=neg_lse[:, t : t + 1])
 
         v_bf = sb("v_bf", [P, N * PACK], BF16, "k_bf")
-        v_first = sb("v_first", [P, 2 * N], BF16)
+        v_first = sb("v_first", [P, 2 * N], BF16, "q_raw")
         gather_on_scalar(v_first[:, 0:N], v_pool[0])
         gather_on_vector(v_first[:, N : N + HALF], v_pool[1], 0, HALF)
         gather_on_scalar(v_first[:, N + HALF : 2 * N], v_pool[1], HALF, N)
@@ -199,7 +198,8 @@ def tile_attend_gat_lse_qk_ts_kernel(
         gather_on_scalar(v_g[:, 0:N], v_pool[2])
         v_mx = mx_tiles("v")
         gather_on_vector(v_g[:, N : N + HALF], v_pool[3], 0, HALF)
-        gather_on_scalar(v_g[:, N + HALF : 2 * N], v_pool[3], HALF, N)
+        gather_on_vector(v_g[:, N + HALF : 2 * N - P], v_pool[3], HALF, N - P)
+        gather_on_scalar(v_g[:, 2 * N - P : 2 * N], v_pool[3], N - P, N)
         for c0 in (0, HALF):
             nc.vector.tensor_copy(*pair_views(v_bf, v_g, 1, c0, c0 + HALF))
         for c0 in (0, HALF):
@@ -229,7 +229,7 @@ def tile_attend_gat_lse_qk_ts_kernel(
 
         ds_bf = sb("ds_bf", [P, PACK * N], BF16)
         ds_planes = ds_bf[:].rearrange("p (t i) -> p t i", t=PACK)
-        dp = [bank("mm") for t in range(PACK)]
+        dp = [bank(t) for t in range(PACK)]
 
         def gradient(t, c0):
             matmul(dp[t][:, c0 : c0 + HALF], do_mx, E5M2, t, v_mx, E4M3, c0, c0 + HALF)
@@ -248,7 +248,7 @@ def tile_attend_gat_lse_qk_ts_kernel(
         dss_mx = mx_tiles("dss")
 
         def turn_gradient(t):
-            turned = bank("turn")
+            turned = bank(TURN + t)
             turn_pairs(turned, 0, ds_bf[:, N * t : N * (t + 1)])
             nc.scalar.copy(
                 laid(dss_bf, P * t, P * (t + 1)).bitcast(F32).rearrange("p (m u) -> p m u", u=2),
@@ -307,16 +307,16 @@ def tile_attend_gat_lse_qk_ts_kernel(
         nc.vector.tensor_copy(*interleave_views(dsr_bf, HALF, N, ds_planes[:, :, HALF:N]))
         quantize_qm(1)
         quantize_block(dsr_mx, E5M2, dsr_bf, 2, 4)
-        query_gradient(nc.vector.tensor_copy, 0, bank("turn"))
+        query_gradient(nc.vector.tensor_copy, 0, bank(TURN))
         key_gradient(nc.scalar.copy, 0, HALF, N, dp[1])
         scatter_on_scalar(0, HALF)
         store_window(0)
         quantize_block(dss_mx, E5M2, dss_bf, 2, 4)
-        query_gradient(nc.vector.tensor_copy, 1, bank("turn"))
+        query_gradient(nc.vector.tensor_copy, 1, bank(TURN + 1))
         quantize_qm(2)
         quantize_qm(3)
         key_gradient(nc.vector.tensor_copy, 1, 0, N, dp[2])
-        query_gradient(nc.vector.tensor_copy, 2, bank("turn"))
+        query_gradient(nc.vector.tensor_copy, 2, bank(TURN + 2))
         scatter_on_vector(1)
         store_window(1)
         key_gradient(nc.scalar.copy, 2, 0, N, dp[1])

from contextlib import ExitStack

import concourse.mybir as mybir
from concourse.masks import make_identity

N, T, D, DV, R = 512, 2048, 512, 512, 512
FLOPS = 2 * R * N * (D + DV + D + D)

F32 = mybir.dt.float32
BF16 = mybir.dt.bfloat16
U32 = mybir.dt.uint32
U16 = mybir.dt.uint16
U8 = mybir.dt.uint8
E4M3 = mybir.dt.float8_e4m3fn_x4
E5M2 = mybir.dt.float8_e5m2_x4
ACT = mybir.ActivationFunctionType
ALU = mybir.AluOpType

P = 128
PACK = 4
WIDTH = 512
HALF = WIDTH // 2
BAND = 16
RUN = 4
QUARTER = P // PACK
TURN = 4


def tile_attend_gat_lse_qk_ts_kernel(
    tc, qT, kT, vT, doT, lse, delta, rw, ts, qm, offs, out_0, out_1
):
    nc = tc.nc
    with ExitStack() as ctx:
        keep = ctx.enter_context(tc.tile_pool(name="keep", bufs=1))
        psum = ctx.enter_context(tc.psum_pool(name="psum", bufs=1))

        def sb(name, shape, dtype, reuse=None):
            return keep.tile(shape, dtype, name=name, tag=reuse or name, align_bytes=64)

        def bank(n):
            return psum.tile([P, WIDTH], F32, name="bank%d" % n, tag="bank%d" % n)

        def mx_tiles(name, reuse=None):
            return sb(name + "_codes", [P, WIDTH], U32, reuse), sb(name + "_scales", [P, WIDTH], U8)

        def quantize(mx, fmt, c0, c1, values):
            nc.vector.quantize_mx(out=mx[0][:, c0:c1].bitcast(fmt), scales=mx[1][:, c0:c1], in_=values)

        def laid(tile, c0, c1):
            return tile[:, PACK * c0 : PACK * c1]

        def matmul(out, stationary, stationary_fmt, block, moving, moving_fmt, c0=0, c1=WIDTH):
            cols = slice(P * block, P * (block + 1))
            nc.tensor.matmul_mx(
                out=out,
                lhsT=stationary[0][:, cols].bitcast(stationary_fmt),
                lhsT_scale=stationary[1][:, cols],
                rhs=moving[0][:, c0:c1].bitcast(moving_fmt),
                rhs_scale=moving[1][:, c0:c1],
                start=True,
                stop=True,
            )

        def gather_on_vector(out, window, c0=0, c1=N):
            nc.vector.tensor_copy(out, window.indirect(offsets[:, c0 // BAND : c1 // BAND]))

        def gather_on_scalar(out, window, c0=0, c1=N):
            nc.scalar.activation(out, window.indirect(offsets[:, c0 // BAND : c1 // BAND]), ACT.Copy)

        def interleave_views(dst, c0, c1, planes):
            out = laid(dst, c0, c1).rearrange("p (c i j) -> p c j i", i=RUN, j=PACK)
            return out, planes.rearrange("p j (c i) -> p c j i", i=RUN)

        def pair_views(dst, pair, h, c0=0, c1=N):
            out = dst[:].rearrange("p (c j) -> p c j", j=PACK)[:, c0:c1, 2 * h : 2 * h + 2]
            return out, pair[:].rearrange("p (j c) -> p c j", j=2)[:, c0:c1]

        def query_views(dst, planes, m0, m1, t0=0, t1=PACK):
            out = dst[:].rearrange("p (t m j) -> p m j t", t=PACK, j=PACK)[:, m0:m1, :, t0:t1]
            return out, planes.rearrange("p j (m t) -> p m j t", t=PACK)[:, :, :, t0:t1]

        offsets = keep.tile([P, N // BAND], U16, name="offsets")
        k_rows = kT.rearrange("(p j) t -> p j t", j=PACK)
        v_rows = vT.rearrange("(p j) t -> p j t", j=PACK)
        k_pair = sb("k_pair", [P, 2 * T], F32)
        k_pool = [k_pair[:, 0:T], k_pair[:, T : 2 * T]] + [sb("k_pool%d" % j, [P, T], F32)[:] for j in (2, 3)]
        v_pool = [sb("v_pool%d" % j, [P, T], F32)[:] for j in range(PACK)]
        q_raw = sb("q_raw", [P, PACK, R], F32)
        do_raw = [sb("do_raw%d" % h, [P, PACK, P], F32) for h in range(PACK)]
        qm_raw = [sb("qm_raw%d" % b, [P, PACK, P], F32) for b in range(PACK)]
        ts_pool = sb("ts_pool", [P, T], F32)
        windows = [sb("window%d" % b, [P, T], F32) for b in range(PACK)]
        for window in windows[:-1]:
            nc.vector.memset(window[:], 0.0)
        ts_raw = sb("ts_raw", [P, T // P], F32)
        lse_c = sb("lse_c", [P, PACK], F32)
        delta_c = sb("delta_c", [P, PACK], F32)
        rw_c = sb("rw_c", [P, PACK], F32)
        nc.scalar.dma_start(ts_raw[:], ts[0].rearrange("(p c) -> p c", p=P))
        for columns, vector in ((lse_c, lse), (rw_c, rw)):
            nc.scalar.dma_start(columns[:], vector[0].rearrange("(p t) o -> p (t o)", t=PACK))
        nc.sync.dma_start(offsets[:], offs)
        nc.sync.dma_start(k_pair[:].rearrange("p (j t) -> p j t", j=2), k_rows[:, 0:2, :])
        for j in (2, 3):
            nc.sync.dma_start(k_pool[j], k_rows[:, j, :])
        nc.sync.dma_start(q_raw[:], qT[0].rearrange("(p j) r -> p j r", j=PACK))
        for j in range(PACK):
            nc.sync.dma_start(v_pool[j], v_rows[:, j, :])
        do_rows = doT[0].rearrange("(p j) r -> p j r", j=PACK)
        for h in range(PACK):
            nc.sync.dma_start(do_raw[h][:], do_rows[:, :, P * h : P * (h + 1)])
        nc.sync.dma_start(delta_c[:], delta[0].rearrange("(p t) o -> p (t o)", t=PACK))
        qm_rows = qm[0].rearrange("(p t) d -> p t d", t=PACK)
        for b in range(PACK):
            nc.sync.dma_start(qm_raw[b][:], qm_rows[:, :, P * b : P * (b + 1)])

        ident = sb("ident", [P, P], F32)
        make_identity(nc, ident[:])
        nc.gpsimd.memset(windows[-1][:], 0.0)

        k_g = [sb("k_g%d" % h, [P, 2 * N], BF16, "ts_pool" if h == 1 else None) for h in range(2)]
        kt_bf = sb("kt_bf", [P, D * PACK], BF16)

        def turn_pairs(turned, column, plane, dealt=False):
            words = plane.bitcast(F32)
            for u in range(2):
                picked = words[:, P * u : P * (u + 1)] if dealt else words[:, u::2]
                nc.tensor.transpose(turned[:, column + P * u : column + P * (u + 1)], picked, ident[:])

        def turn_keys(h):
            turned = bank(TURN + 3 - 3 * h)
            for e in range(2):
                turn_pairs(turned, HALF * e, k_g[h][:, N * e : N * (e + 1)], dealt=h == 0)
            nc.scalar.copy(
                laid(kt_bf, HALF * h, HALF * (h + 1)).bitcast(F32).rearrange("m (e p u) -> m e p u", e=2, u=2),
                turned[:].rearrange("m (e u p) -> m e p u", e=2, u=2),
            )

        def gather_dealt_plane(j):
            gather_on_vector(k_g[0][:, N * j : N * (j + 1)].rearrange("p (u m e) -> p m u e", u=2, e=2), k_pool[j])

        neg_lse = sb("neg_lse", [P, PACK], F32)
        nc.vector.tensor_scalar(neg_lse[:], lse_c[:], -1.0, None, ALU.mult)
        ts_places = ts_pool[:].rearrange("m (p c) -> m p c", p=P)
        for c0 in range(0, T // P, PACK):
            turned = bank(TURN + c0 // PACK)
            for c in range(PACK):
                column = ts_raw[:, c0 + c : c0 + c + 1].to_broadcast([P, P])
                nc.tensor.transpose(turned[:, P * c : P * (c + 1)], column, ident[:])
            nc.scalar.copy(ts_places[:, :, c0 : c0 + PACK], turned[:].rearrange("m (c p) -> m p c", c=PACK))
        ts_row = sb("ts_row", [P, N], F32)
        gather_on_scalar(ts_row[:], ts_pool[:])
        gather_dealt_plane(0)
        gather_dealt_plane(1)
        turn_keys(0)
        k_bf = sb("k_bf", [P, N * PACK], BF16)
        nc.vector.tensor_copy(
            k_bf[:].rearrange("p (m u e j) -> p m u e j", u=2, e=2, j=PACK)[:, :, :, :, 0:2],
            k_g[0][:].rearrange("p (j u m e) -> p m u e j", j=2, u=2, e=2),
        )
        gather_on_vector(k_g[1][:, 0:N], k_pool[2])
        gather_on_vector(k_g[1][:, N : N + HALF], k_pool[3], 0, HALF)
        gather_on_scalar(k_g[1][:, N + HALF : 2 * N], k_pool[3], HALF, N)
        turn_keys(1)
        k_mx = mx_tiles("k")
        nc.vector.tensor_copy(*pair_views(k_bf, k_g[1], 1))
        quantize(k_mx, E4M3, 0, N, k_bf[:])
        kt_mx = mx_tiles("kt")
        quantize(kt_mx, E4M3, 0, D, kt_bf[:])

        q_bf = sb("q_bf", [P, R * PACK], BF16, "k_g0")
        q_mx = mx_tiles("q")
        for h in range(2):
            nc.scalar.copy(*query_views(q_bf, q_raw[:], 0, P, 2 * h, 2 * h + 2))
        for t in range(PACK):
            quantize(q_mx, E4M3, P * t, P * (t + 1), laid(q_bf, P * t, P * (t + 1)))

        a_sb = [sb("a_sb%d" % t, [P, N], F32) for t in range(PACK)]
        p_sb = [sb("p_sb%d" % t, [P, N], F32) for t in range(PACK)]
        for t in range(PACK):
            scores = bank(t)
            matmul(scores[:], q_mx, E4M3, t, k_mx, E4M3)
            nc.vector.tensor_tensor(a_sb[t][:], scores[:], ts_row[:], ALU.mult)
            nc.scalar.activation(p_sb[t][:], a_sb[t][:], ACT.Exp, bias=neg_lse[:, t : t + 1])

        v_bf = sb("v_bf", [P, N * PACK], BF16, "k_bf")
        v_first = sb("v_first", [P, 2 * N], BF16, "q_raw")
        gather_on_scalar(v_first[:, 0:N], v_pool[0])
        gather_on_vector(v_first[:, N : N + HALF], v_pool[1], 0, HALF)
        gather_on_scalar(v_first[:, N + HALF : 2 * N], v_pool[1], HALF, N)
        nc.vector.tensor_copy(*pair_views(v_bf, v_first, 0))
        w_sb = sb("w_sb", [P, PACK * N], F32, "ts_pool")
        for t in range(PACK):
            nc.vector.scalar_tensor_tensor(
                w_sb[:, N * t : N * (t + 1)], p_sb[t][:], rw_c[:, t : t + 1], ts_row[:], ALU.mult, ALU.mult
            )
        v_g = sb("v_g", [P, 2 * N], BF16, "neg_lse")
        gather_on_scalar(v_g[:, 0:N], v_pool[2])
        v_mx = mx_tiles("v")
        gather_on_vector(v_g[:, N : N + HALF], v_pool[3], 0, HALF)
        gather_on_vector(v_g[:, N + HALF : 2 * N - P], v_pool[3], HALF, N - P)
        gather_on_scalar(v_g[:, 2 * N - P : 2 * N], v_pool[3], N - P, N)
        for c0 in (0, HALF):
            nc.vector.tensor_copy(*pair_views(v_bf, v_g, 1, c0, c0 + HALF))
        for c0 in (0, HALF):
            quantize(v_mx, E4M3, c0, c0 + HALF, laid(v_bf, c0, c0 + HALF))

        do_bf = sb("do_bf", [P, R * PACK], BF16)
        do_mx = mx_tiles("do")
        for h in range(2):
            nc.scalar.copy(*query_views(do_bf, do_raw[h][:], QUARTER * h, QUARTER * (h + 1)))
        for t0 in (0, 2):
            for h in range(2, PACK):
                nc.scalar.copy(*query_views(do_bf, do_raw[h][:], QUARTER * h, QUARTER * (h + 1), t0, t0 + 2))
        for t in range(PACK):
            quantize(do_mx, E5M2, P * t, P * (t + 1), laid(do_bf, P * t, P * (t + 1)))

        qm_bf = [sb("qm_bf%d" % b, [P, P * PACK], BF16, "do_bf" if b == 1 else None) for b in range(PACK)]
        qm_mx = mx_tiles("qm")

        def lay_qm(b):
            nc.scalar.copy(*interleave_views(qm_bf[b], 0, P, qm_raw[b][:]))

        def quantize_qm(b):
            quantize(qm_mx, E4M3, P * b, P * (b + 1), qm_bf[b][:])

        def quantize_block(mx, fmt, tile, b0, b1):
            quantize(mx, fmt, P * b0, P * b1, laid(tile, P * b0, P * b1))

        ds_bf = sb("ds_bf", [P, PACK * N], BF16)
        ds_planes = ds_bf[:].rearrange("p (t i) -> p t i", t=PACK)
        dp = [bank(t) for t in range(PACK)]

        def gradient(t, c0):
            matmul(dp[t][:, c0 : c0 + HALF], do_mx, E5M2, t, v_mx, E4M3, c0, c0 + HALF)
            nc.vector.scalar_tensor_tensor(
                ds_bf[:, N * t + c0 : N * t + c0 + HALF],
                dp[t][:, c0 : c0 + HALF],
                delta_c[:, t : t + 1],
                w_sb[:, N * t + c0 : N * t + c0 + HALF],
                ALU.subtract,
                ALU.mult,
            )

        dsr_bf = sb("dsr_bf", [P, N * PACK], BF16)
        dsr_mx = mx_tiles("dsr")
        dss_bf = sb("dss_bf", [P, R * PACK], BF16)
        dss_mx = mx_tiles("dss")

        def turn_gradient(t):
            turned = bank(TURN + t)
            turn_pairs(turned, 0, ds_bf[:, N * t : N * (t + 1)])
            nc.scalar.copy(
                laid(dss_bf, P * t, P * (t + 1)).bitcast(F32).rearrange("p (m u) -> p m u", u=2),
                turned[:, 0 : 2 * P].rearrange("p (u m) -> p m u", u=2),
            )

        dk_sb = [sb("dk_sb%d" % b, [P, N], F32) for b in range(PACK)]
        gq_sb = [sb("gq_sb%d" % t, [P, D], F32) for t in range(PACK)]
        gq_rows = out_0[0].rearrange("(m t) d -> m t d", t=PACK)

        def key_gradient(copy, b, c0, c1, dk):
            matmul(dk[:, c0:c1], qm_mx, E4M3, b, dsr_mx, E5M2, c0, c1)
            copy(dk_sb[b][:, c0:c1], dk[:, c0:c1])

        def places(b, c0, c1):
            return windows[b][:].indirect(offsets[:, c0 // BAND : c1 // BAND])

        def scatter_on_scalar(b, c0):
            nc.scalar.activation(places(b, c0, c0 + HALF), dk_sb[b][:, c0 : c0 + HALF], ACT.Copy)

        def scatter_on_vector(b):
            nc.vector.tensor_copy(places(b, 0, N), dk_sb[b][:])

        def store_window(b):
            nc.sync.dma_start(out_1[P * b : P * (b + 1), :], windows[b][:])

        def query_gradient(copy, t, gq):
            matmul(gq[:], dss_mx, E5M2, t, kt_mx, E4M3)
            copy(
                gq_sb[t][:].rearrange("m (p j) -> m p j", j=PACK),
                gq[:].rearrange("m (j p) -> m p j", j=PACK),
            )
            nc.scalar.dma_start(gq_rows[:, t, :], gq_sb[t][:])

        for b in (0, 2, 3):
            lay_qm(b)
        nc.gpsimd.tensor_scalar(*interleave_views(qm_bf[1], 0, P, qm_raw[1][:]), 1.0, 0.0, ALU.mult, ALU.add)
        for t in range(PACK):
            gradient(t, 0)
        quantize_qm(0)
        nc.vector.tensor_copy(*interleave_views(dsr_bf, 0, P, ds_planes[:, :, 0:P]))
        nc.scalar.copy(*interleave_views(dsr_bf, P, HALF, ds_planes[:, :, P:HALF]))
        quantize_block(dsr_mx, E5M2, dsr_bf, 0, 1)
        quantize_block(dsr_mx, E5M2, dsr_bf, 1, 2)
        gradient(0, HALF)
        gradient(1, HALF)
        key_gradient(nc.scalar.copy, 0, 0, HALF, dp[0])
        turn_gradient(0)
        scatter_on_scalar(0, 0)
        gradient(2, HALF)
        gradient(3, HALF)
        turn_gradient(1)
        turn_gradient(2)
        turn_gradient(3)
        quantize_block(dss_mx, E5M2, dss_bf, 0, 2)
        nc.vector.tensor_copy(*interleave_views(dsr_bf, HALF, N, ds_planes[:, :, HALF:N]))
        quantize_qm(1)
        quantize_block(dsr_mx, E5M2, dsr_bf, 2, 4)
        query_gradient(nc.vector.tensor_copy, 0, bank(TURN))
        key_gradient(nc.scalar.copy, 0, HALF, N, dp[1])
        scatter_on_scalar(0, HALF)
        store_window(0)
        quantize_block(dss_mx, E5M2, dss_bf, 2, 4)
        query_gradient(nc.vector.tensor_copy, 1, bank(TURN + 1))
        quantize_qm(2)
        quantize_qm(3)
        key_gradient(nc.vector.tensor_copy, 1, 0, N, dp[2])
        query_gradient(nc.vector.tensor_copy, 2, bank(TURN + 2))
        scatter_on_vector(1)
        store_window(1)
        key_gradient(nc.scalar.copy, 2, 0, N, dp[1])
        query_gradient(nc.scalar.copy, PACK - 1, dp[3])
        for c0 in (0, HALF):
            scatter_on_scalar(2, c0)
        store_window(2)
        key_gradient(nc.vector.tensor_copy, 3, 0, N, dp[2])
        scatter_on_vector(3)
        store_window(3)
